import numpy as np, ml_dtypes
CORES = [2,6,10,14,18,22,26,30]
N = 8
BF = ml_dtypes.bfloat16
def gentries(a):
    return np.ascontiguousarray(a.reshape(8, 16, -1).transpose(0, 2, 1)).reshape(8, -1)
def gtable(e):
    e = np.asarray(e); return np.ascontiguousarray(e.reshape(8, -1, 16).transpose(0, 2, 1)).reshape(128, -1).astype(np.int32)
def f(rng, *shape):
    return (rng.standard_normal(shape, dtype=np.float32) * np.exp2(rng.integers(-2, 3, shape[:-1] + (1,)))).astype(BF)
def wide(rng, *shape):
    v = f(rng, *shape).astype(np.float32); k = shape[:-2] + (1, shape[-1])
    return (v * np.exp2(rng.integers(-6, 7, k)) * (rng.random(k) > 0.0625)).astype(BF)
M, S, D, Q = 2048, 32, 16, 4
P = N // Q
def forest(rng, L, aside, bushy, zero=False):
    free = S + rng.permutation(M - S); n = S * (D - 1)
    chain = np.concatenate([np.arange(S)[:, None], free[:n].reshape(S, D - 1)], 1)
    p = np.arange(M); dep = np.full(M, -1); dep[chain] = np.arange(D); p[chain[:, 1:]] = chain[:, :-1]; rest = free[n:]
    if bushy:
        h = len(rest) // 2; p[rest[:h]] = rng.integers(0, S); p[rest[h:]] = chain[rng.integers(0, S), D - 2]
    else:
        lev = rng.integers(1, D, len(rest))
        for d in range(1, D):
            v = rest[lev == d]; p[v] = rng.choice(np.flatnonzero(dep == d - 1), len(v)); dep[v] = d
    kids = S + rng.permutation(M - S); o = kids[np.argsort(p[kids], kind="stable")]; q = p[o]
    sib = np.zeros(M, np.int64); sib[o] = np.arange(M - S) - np.searchsorted(q, q); c = np.bincount(q, minlength=M)
    base = rng.integers(0, 4096, M); step = 2 * rng.integers(0, 2048, M) + 1
    if zero: base[0] = 0
    x = np.where((c > 0) & (rng.random(M) < 0.7), (rng.random(M) * c).astype(np.int64), c + (rng.random(M) * (4096 - c)).astype(np.int64))
    x[chain[:, :-1]] = sib[chain[:, 1:]]
    e = np.flatnonzero(L < D - 1); b = chain[e, L[e]]; w = sib[chain[e, L[e] + 1]]; cb = c[b]
    other = (w + 1 + (rng.random(len(e)) * (cb - 1)).astype(np.int64)) % cb; none = cb + (rng.random(len(e)) * (4096 - cb)).astype(np.int64)
    x[b] = np.where((cb > 1) & (rng.random(len(e)) < aside), other, none)
    t = (base + step * x) % 4096
    k = np.zeros(M, np.int64); k[o] = (base[q] + step[q] * sib[o]) % 4096
    k[:S] = np.where(rng.random(S) < 0.5, t[:S], rng.integers(0, 4096, S))
    return p, k, t
def shards(rng, t, sc, tie):
    v = sc * 4096 + t; win = rng.integers(0, N, t.shape); u = rng.random((N,) + t.shape)
    o = np.where(rng.random(t.shape) < tie, sc * 4096 + (u * (t + 1)).astype(np.int64), (u * (v + 1)).astype(np.int64))
    o = np.where((np.arange(N)[:, None, None, None] == win) | (rng.random(o.shape) < 0.03125), v, np.minimum(o, v))
    return np.ascontiguousarray(o.transpose(0, 2, 1, 3)).reshape(N, 8, N * M).astype(np.int32)
def draw(rng, L, aside=0.5, bushy=False, tie=0.125, uneven=False, zero=False):
    a = [[forest(rng, L[q, g], aside, bushy, zero) for g in range(8)] for q in range(N)]
    p, k, t = [np.array([[a[q][g][i] for g in range(8)] for q in range(N)]) for i in range(3)]
    sc = rng.integers(0, 4096, t.shape)
    if uneven: sc = 4095 >> rng.integers(0, 13, t.shape)
    return {"par": np.stack([gtable(p[q]) for q in range(N)]), "tok": k.astype(np.int32), "best": shards(rng, t, sc, tie), "kv": f(rng, N, 128, Q * M)}
def setup_inputs(rng):
    return draw(rng, rng.integers(0, D, (N, 8, S)))
def setup_inputs_full(rng):
    return draw(rng, np.full((N, 8, S), D - 1))
def setup_inputs_cut(rng):
    return draw(rng, rng.choice(np.array([0, 1, D - 2]), (N, 8, S)), aside=0.0, zero=True)
def setup_inputs_ties(rng):
    return draw(rng, rng.integers(0, D, (N, 8, S)), tie=1.0)
def setup_inputs_bushy(rng):
    return draw(rng, rng.integers(0, D, (N, 8, S)), bushy=True)
def setup_inputs_spread(rng):
    d = draw(rng, rng.integers(0, D, (N, 8, S)), uneven=True); d["kv"] = wide(rng, N, 128, Q * M); return d
def check_inputs(d):
    bad = []; p = np.stack([gentries(a) for a in d["par"]]).astype(np.int64); k = d["tok"].astype(np.int64); b = d["best"]
    if not np.isfinite(d["kv"].astype(np.float32)).all(): bad.append("finite")
    if b.min() < 0 or b.max() >= 1 << 24: bad.append("best")
    if k.min() < 0 or k.max() > 4095: bad.append("tokens")
    if p.min() < 0 or p.max() >= M: return bad + ["parents"]
    if (p[:, :, :S] != np.arange(S)).any(): bad.append("roots")
    a = p
    for i in range(D - 2): a = np.take_along_axis(p, a, 2)
    if (a >= S).any(): bad.append("depth")
    w = np.sort((p * 4096 + k)[:, :, S:], axis=2)
    if (w[:, :, 1:] == w[:, :, :-1]).any(): bad.append("children")
    return bad
def reference(par, tok, best, kv):
    p = np.stack([gentries(a) for a in par]).astype(np.int64)
    t = np.max(best, axis=0).reshape(8, N, M).transpose(1, 0, 2) & 4095
    ok = (np.arange(M) < S) | (tok == np.take_along_axis(t, p, 2))
    a = np.broadcast_to(np.arange(M), p.shape); acc = np.ones(p.shape, bool); dep = np.zeros(p.shape, np.int64)
    for i in range(D):
        acc = acc & np.take_along_axis(ok, a, 2); dep = dep + (a >= S); a = np.take_along_axis(p, a, 2)
    y = np.zeros((N, 128, Q * S * D), BF)
    for r in range(N):
        out = y[r].reshape(8, 16, Q * S * D)
        for i in range(Q):
            q = P * i + r % P; k = kv[r][:, i * M:(i + 1) * M].reshape(8, 16, M)
            g, j = np.nonzero(acc[q])
            out[g, :, (i * S + a[q, g, j]) * D + dep[q, g, j]] = k[g, :, j]
    return {"y": y}

@@ -1,0 +1,325 @@
+from concourse.bass import DstId, RemoteDMATransfer
+from concourse.mybir import AluOpType as A, ActivationFunctionType as AF
+
+M, S, D, Q = 2048, 32, 16, 4
+Z = 16
+W = M + Z
+H = M // 2
+PIECES = [(2, 16), (16, 48), (48, 80), (80, 128)]
+
+SCRATCH = {
+    "dsc": ("dram", [8, 128, 128], "int32"),
+    "land": ("sbuf", [128, 1024], "int32"),
+    "parw": ("sbuf", [128, 128], "int32"),
+    "tokc": ("sbuf", [128, 128], "int32"),
+    "it1": ("sbuf", [128, 128], "int32"),
+    "it2": ("sbuf", [128, 128], "int32"),
+    "acc": ("sbuf", [128, 128], "int32"),
+    "tgt": ("sbuf", [128, 128], "int32"),
+    "pcol": ("sbuf", [128, 1], "int32"),
+    "pa": ("sbuf", [128, 1], "int32"),
+    "pg": ("sbuf", [128, 1], "int32"),
+    "cst": ("sbuf", [128, 16], "float32"),
+    "mg": ("sbuf", [128, 128], "float32"),
+    "strip": ("sbuf", [128, 144], "float32"),
+    "step": ("sbuf", [128, 32], "float32"),
+    "bm": ("sbuf", [128, 128], "float16"),
+    "bk2": ("sbuf", [128, 128], "float16"),
+    "em": ("sbuf", [128, 2048], "float16"),
+    "fm": ("sbuf", [128, 144], "bfloat16"),
+    "fh": ("sbuf", [128, 144], "float16"),
+    "tokh": ("sbuf", [128, 128], "float16"),
+    "hiw": ("sbuf", [128, 128], "float16"),
+    "lst": ("sbuf", [128, 128], "uint16"),
+    "pars": ("sbuf", [128, 128], "float32"),
+    "ktmp": ("sbuf", [128, 2048], "float32"),
+    "kk": ("sbuf", [128, 2048], "float32"),
+    "eq": ("sbuf", [128, 2048], "bfloat16"),
+    "offu": ("sbuf", [128, 128], "uint16"),
+    "vals": ("sbuf", [128, 2048], "float32"),
+    "nxt": ("sbuf", [128, W + M], "float32"),
+    "c16": ("sbuf", [128, 128], "bfloat16"),
+    "arow": ("sbuf", [128, 128], "bfloat16"),
+    "ones": ("sbuf", [128, 128], "bfloat16"),
+    "mask": ("sbuf", [128, 32], "float32"),
+    "res": ("sbuf", [128, 16], "bfloat16"),
+    "md": ("sbuf", [128, 32 * D], "float16"),
+    "offw": ("sbuf", [128, 32 * D + 32], "uint16"),
+    "lu": ("sbuf", [128, 32], "uint16"),
+    "lists": ("sbuf", [128, 32 * Q], "uint16"),
+    "kvw": ("sbuf", [128, W * Q], "bfloat16"),
+    "ysb": ("sbuf", [128, 512 * Q], "bfloat16"),
+    "psA": ("psum", [128, 2048], "float32"),
+    "psB": ("psum", [128, 2048], "float32"),
+}
+SEMAPHORES = ["vs", "ss", "ps", "gs", "ldD", "ldS", "ldM", "ldP", "ldO", "ldpar", "ldtok", "ldk0", "ldk1", "ldk2", "ldk3",
+              "sent", "aD", "aS", "aM", "aP", "lsent", "li0", "li1", "li2", "li3", "stored"]
+
+
+def rank_program(g, core, T, topo):
+    rank = T.rank_of(core)
+    if rank is None:
+        return
+    eng = {"v": g.vector, "s": g.scalar, "p": g.tensor, "g": g, "y": g.sync}
+    semof = {"v": "vs", "s": "ss", "p": "ps", "g": "gs"}
+    count = {"v": 0, "s": 0, "p": 0, "g": 0}
+    seen = {}
+
+    def need(q, deps):
+        for name, val in deps:
+            if seen.get((q, name), 0) < val:
+                eng[q].wait_ge(T.sem[name], int(val))
+                seen[(q, name)] = val
+
+    def done(q, ins):
+        count[q] += 1
+        ins.then_inc(T.sem[semof[q]], 1)
+        return (semof[q], count[q])
+
+    chip = topo.chip(core)
+    same, mate, plane, diag = [], [], [], []
+    for c in T.cores:
+        if c == core:
+            continue
+        oc = topo.chip(c)
+        if oc == chip:
+            same.append(c)
+        elif topo.mates(chip, oc):
+            mate.append(c)
+        elif topo.same_plane(chip, oc):
+            plane.append(c)
+        else:
+            diag.append(c)
+    off = topo.engines(core, diag[0])
+    half = len(off) // 2
+    bits = lambda es: sum(1 << e for e in es)
+    inner = [e for e in topo.engines(core, same[0]) if e not in off]
+
+    def dst_id(c):
+        a = topo.addr(c)
+        return DstId(rid=a[0], pnc=a[1])
+
+    slot = lambda r: T.land[:, r * 128:(r + 1) * 128]
+    piece = lambda r: T.best[:, r * M:(r + 1) * M]
+    blk = lambda k: slice(k * 128, (k + 1) * 128)
+    R = T.rank_of
+
+    stage = lambda q, c, sem: q.dma_start(T.dsc[R(c)], piece(R(c))).then_inc(T.sem[sem], 16)
+    for c in diag:
+        stage(g.sync, c, "ldD")
+    for c in plane:
+        stage(g.sync, c, "ldS")
+    g.sync.dma_start(slot(rank), piece(rank)).then_inc(T.sem.ldO, 16)
+    stage(g.scalar, same[0], "ldP")
+    g.scalar.dma_start(T.tokc[:], T.tok[:]).then_inc(T.sem.ldtok, 16)
+    g.scalar.dma_start(T.parw[:], T.par[:]).then_inc(T.sem.ldpar, 16)
+    for c in mate:
+        stage(g.scalar, c, "ldM")
+
+    loose = dict(allow_small_or_imprecise_dtypes=True)
+    i_p = done("g", g.iota(T.pcol[:], [[1, 1]], 0, 1))
+    i_mg = done("g", g.iota(T.mg[:], [[1, 8], [0, 16]], 0, 0, **loose))
+    i_strip = done("g", g.iota(T.strip[:], [[1, 144]], 0, 0, **loose))
+    need("g", [("ldP", 16)])
+    g.remote_dma_fused([RemoteDMATransfer(dst_ids=[dst_id(same[0])], dma_engine_mask=bits(inner),
+                                          remote_sem=T.sem.aP, src=T.dsc[R(same[0])], dst=slot(rank))],
+                       local_sem=T.sem.sent)
+    for grp, ld, ar in ((diag, "ldD", "aD"), (plane, "ldS", "aS"), (mate, "ldM", "aM")):
+        need("g", [(ld, 32)])
+        g.remote_dma_fused([RemoteDMATransfer(dst_ids=[dst_id(c)], dma_engine_mask=bits(off[k * half:(k + 1) * half]),
+                                              remote_sem=T.sem[ar], src=T.dsc[R(c)], dst=slot(rank))
+                            for k, c in enumerate(grp)], local_sem=T.sem.sent)
+    done("g", g.iota(T.c16[:], [[16, 128]], W, 0, **loose))
+    i_ar = done("g", g.iota(T.arow[:], [[0, 8], [1, 16]], 0, 0, **loose))
+    i_val = []
+    for n, (ca, cb) in enumerate(PIECES):
+        j = 16 * ca if n else 0
+        i_val.append(done("g", g.iota(T.vals[:, j:16 * cb], [[1, 16 * cb - j]], 1 + j, 0, **loose)))
+    i_step = done("g", g.iota(T.step[:], [[0, 2], [1, 16]], 0, 0, **loose))
+
+    me = rank // 2
+    heads = [c for c in diag + plane + mate if R(c) % 2 == rank % 2]
+    order = [None] + [c for c in mate + plane + diag if c in heads]
+    member = lambda c: me if c is None else R(c) // 2
+    need("y", [("sent", 6 * half + len(inner))])
+    for c in order:
+        i = member(c)
+        g.sync.dma_start(T.kvw[:, i * W + Z:(i + 1) * W], T.kv[:, i * M:(i + 1) * M]).then_inc(T.sem["ldk%d" % i], 16)
+
+    v, t, s = g.vector, g.tensor, g.scalar
+    col = lambda k: T.cst[:, k:k + 1]
+
+    need("v", [i_p])
+    b = done("v", v.tensor_scalar(T.pg[:], T.pcol[:], 4, None, A.arith_shift_right))
+    a = done("v", v.tensor_scalar(T.pa[:], T.pcol[:], 15, None, A.bitwise_and))
+    need("v", [b])
+    c0 = done("v", v.tensor_copy(col(2), T.pg[:]))
+    need("v", [a])
+    done("v", v.tensor_scalar(col(1), T.pa[:], 1.0, None, A.add))
+    done("v", v.tensor_copy(col(0), T.pa[:]))
+    need("v", [c0, i_mg])
+    x = done("v", v.tensor_scalar(T.bm[:], T.mg[:], col(2), None, A.is_equal))
+    need("v", [x])
+    x = done("v", v.tensor_scalar(T.bk2[:], T.bm[:], col(1), None, A.mult))
+    kb = done("v", v.tensor_scalar(col(3), col(0), -4096.0, 2048.0, A.mult, A.add))
+    done("v", v.memset(T.res[:], 1.0))
+    need("v", [x])
+    for k in range(16):
+        done("v", v.tensor_scalar(T.em[:, blk(k)], T.bk2[:], float(k + 1), None, A.is_equal))
+    need("v", [("ldtok", 16)])
+    v_tok = done("v", v.tensor_scalar(T.tokh[:], T.tokc[:], -2048.0, None, A.add))
+    need("v", [("ldpar", 16)])
+    x1 = done("v", v.tensor_scalar(T.it1[:], T.parw[:], 1920, None, A.bitwise_and))
+    x2 = done("v", v.tensor_scalar(T.it2[:], T.parw[:], 127, None, A.bitwise_and))
+    need("v", [x1])
+    v_hi = done("v", v.tensor_scalar(T.hiw[:], T.it1[:], 32.0, None, A.mult))
+    need("v", [x2])
+    done("v", v.tensor_copy(T.lst[:], T.it2[:]))
+    done("v", v.tensor_scalar(T.pars[:], T.parw[:], 1.0, None, A.add))
+    c5 = done("v", v.tensor_scalar(col(5), col(2), 16.0, 15.0, A.mult, A.add))
+    v_ones = done("v", v.memset(T.ones[:], 1.0 / 128))
+    need("v", [c5, i_strip])
+    v_f = done("v", v.tensor_scalar(T.fm[:], T.strip[:], col(5), -8192.0, A.is_equal, A.mult))
+    v_fh = done("v", v.tensor_scalar(T.fh[:], T.strip[:], col(5), None, A.is_equal))
+    lcol = lambda d, h: 32 * d + 16 * h + 16
+    last = [done("v", v.tensor_scalar(T.offw[:, lcol(0, h):lcol(0, h) + 1], col(0), float(1 + 16 * h), None, A.add))
+            for h in range(2)]
+    for i in range(Q):
+        done("v", v.memset(T.kvw[:, i * W:i * W + Z], 0.0))
+
+    pa_done, pb_done = [], []
+    for hf in range(2):
+        need("p", [v_tok])
+        for bank in (2 * hf, 2 * hf + 1):
+            for k in range(4 * bank, 4 * bank + 4):
+                ins = t.matmul(T.psA[:, blk(k)], T.em[:, blk(k)], T.tokh[:], True, True)
+            pa_done.append(done("p", ins))
+        need("p", [v_hi])
+        for bank in range(2):
+            for k in range(8 * bank, 8 * bank + 8):
+                o = H * hf + 64 * k
+                ins = t.matmul(T.psB[:, o:o + 64], T.em[:, blk(k)], T.hiw[:, 64 * hf:64 * hf + 64], True, True)
+            pb_done.append(done("p", ins))
+
+    need("s", [i_mg])
+    done("s", s.activation(T.nxt[:, M:W], T.mg[:, 0:Z], AF.Silu, scale=0.0))
+    ks = []
+    for bank in range(4):
+        need("s", [pa_done[bank], kb])
+        cs = slice(bank * 512, (bank + 1) * 512)
+        ks.append(done("s", s.activation(T.ktmp[:, cs], T.psA[:, cs], AF.Identity, bias=col(3), scale=1.0)))
+    need("s", ks)
+    s_zero = done("s", s.activation(T.nxt[:, 0:M], T.ktmp[:], AF.Identity, scale=0.0))
+
+    def ksum(hf):
+        out = []
+        need("v", [ks[2 * hf], ks[2 * hf + 1]])
+        for k in range(16):
+            need("v", [pb_done[2 * hf + k // 8]])
+            o, js = H * hf + 64 * k, slice(H * hf + k, H * hf + H, 16)
+            out.append(done("v", v.tensor_tensor(T.kk[:, js], T.psB[:, o:o + 64], T.ktmp[:, js], A.add)))
+        return out
+
+    v_kA = ksum(0)
+
+    need("p", [v_ones, v_f, i_ar] + ks)
+    for n, (ca, cb) in enumerate(PIECES):
+        ps = T.psA[:, n * 512:n * 512 + cb - ca]
+        t.matmul(ps, T.ones[:], T.c16[:, ca:cb], True, False)
+        t.matmul(ps, T.arow[:], T.ones[:, 0:cb - ca], False, False)
+
+    def both(op, deps=((), ())):
+        out = []
+        for h in range(2):
+            need("v", deps[h])
+            out.append([done("v", op(slice(64 * h, 64 * h + 64)))])
+        return out
+
+    def top(o, p, q, deps=((), ())):
+        return both(lambda c: v.tensor_tensor(o(c), p(c), q(c), A.max), deps)
+
+    part = lambda r: (lambda c: T.land[:, r * 128 + c.start:r * 128 + c.stop])
+    acc, full = (lambda c: T.psB[:, 512 + c.start:512 + c.stop]), (lambda c: T.acc[:, c])
+    need("v", [v_kA[9], ("ldO", 16), ("aP", len(inner))])
+    x = top(acc, part(rank), part(R(same[0])))
+    for grp, ar in ((diag, "aD"), (plane, "aS"), (mate, "aM")):
+        if grp is plane:
+            v_k = ksum(1)[-1]
+        need("v", [(ar, 2 * half)])
+        for c in grp:
+            x = top(full if c == mate[-1] else acc, acc, part(R(c)), x)
+    x = both(lambda c: v.tensor_scalar(T.tgt[:, c], T.acc[:, c], 4095, None, A.bitwise_and), x)
+    need("v", x[1] + [v_k])
+
+    p_ok = []
+
+    def fit(n):
+        ca, cb = PIECES[n]
+        e = done("v", v.tensor_tensor(T.eq[:, 16 * ca:16 * cb], T.tgt[:].indirect(T.lst[:, ca:cb]), T.kk[:, 16 * ca:16 * cb], A.is_equal))
+        need("p", [e])
+        for k in range(16):
+            ins = t.matmul(T.psA[:, n * 512:n * 512 + cb - ca], T.fm[:, 15 - k:143 - k], T.eq[:, 16 * ca + k:16 * cb:16], False, k == 15)
+        p_ok.append(done("p", ins))
+
+    scat = [s_zero]
+
+    def place(n):
+        ca, cb = PIECES[n]
+        need("v", [p_ok[n]])
+        o = done("v", v.tensor_tensor(T.offu[:, ca:cb], T.psA[:, n * 512:n * 512 + cb - ca], T.pars[:, ca:cb], A.max))
+        need("s", [o, i_val[n], scat[-1]])
+        scat.append(done("s", s.activation(T.nxt[:].indirect(T.offu[:, ca:cb]), T.vals[:, 16 * ca:16 * cb], AF.Silu)))
+
+    fit(0)
+    for n in range(1, len(PIECES)):
+        fit(n)
+        place(n - 1)
+    place(len(PIECES) - 1)
+
+    need("v", [i_step])
+    x = done("v", v.tensor_scalar(T.mask[:], T.step[:], col(0), None, A.is_equal))
+    need("v", [x])
+    v_m0 = done("v", v.tensor_tensor(T.md[:, 0:32], T.mask[:], T.vals[:, 0:32], A.mult))
+
+    def collect(d, dep):
+        need("p", [dep, v_fh, v_k])
+        ins = t.matmul(T.psB[:, 0:32], T.fh[:, 15 - d:143 - d], T.md[:, 32 * d:32 * d + 32], d == 0, d == D - 1)
+        return done("p", ins) if d == D - 1 else None
+
+    collect(0, v_m0)
+    need("v", [scat[-1]])
+    for d in range(1, D):
+        xs = []
+        for h in range(2):
+            need("v", [last[h]])
+            b = lcol(d - 1, h)
+            xs.append(done("v", v.tensor_tensor(T.md[:, 32 * d + 16 * h:32 * d + 16 * h + 16],
+                                                T.nxt[:, 0:W].indirect(T.offw[:, b:b + 1]), T.mask[:, 0:16], A.mult)))
+        p_l = collect(d, xs[1])
+        if d < D - 1:
+            for h in range(2):
+                need("v", [xs[h]])
+                b = lcol(d, h)
+                last[h] = done("v", v.tensor_tensor_scan(T.offw[:, b - 15:b + 1], T.res[:],
+                                                         T.md[:, 32 * d + 16 * h:32 * d + 16 * h + 16], 0.0, A.mult, A.add))
+    need("v", [p_l])
+    v_lu = done("v", v.tensor_scalar(T.lu[:], T.psB[:, 0:32], float(Z - 1), None, A.add))
+
+    need("g", [v_lu])
+    mine = T.lists[:, me * 32:(me + 1) * 32]
+    g.remote_dma_fused([RemoteDMATransfer(dst_ids=[dst_id(c) for c in heads], dma_engine_mask=bits(off), remote_sem=T.sem["li%d" % me],
+                                          srcs=[T.lu[:]], dsts=[mine for c in heads], alu_op=0)], local_sem=T.sem.lsent)
+
+    for c in order:
+        i = member(c)
+        win = T.kvw[:, i * W:(i + 1) * W]
+        src = T.lu if c is None else T.lists
+        b0 = 0 if c is None else 32 * i
+        for q in "vs":
+            need(q, [("ldk%d" % i, 16), v_lu] + ([("li%d" % i, len(off))] if c is not None else []))
+        e1 = done("v", v.tensor_copy(T.ysb[:, i * 512:i * 512 + 256], win.indirect(src[:, b0:b0 + 16])))
+        e2 = done("s", s.activation(T.ysb[:, i * 512 + 256:(i + 1) * 512], win.indirect(src[:, b0 + 16:b0 + 32]), AF.Copy))
+        need("y", [e1, e2])
+        g.sync.dma_start(T.y[:, i * 512:(i + 1) * 512], T.ysb[:, i * 512:(i + 1) * 512]).then_inc(T.sem.stored, 16)
+    need("g", [("lsent", len(off)), ("gs", count["g"]), ("ps", count["p"])])
+    need("y", [("stored", 16 * Q)])

@@ -4,11 +4,17 @@ from concourse.mybir import AluOpType as A, ActivationFunctionType as AF
 M, S, D, Q = 2048, 32, 16, 4
 Z = 16
 W = M + Z
-H = M // 2
-PIECES = [(2, 16), (16, 48), (48, 80), (80, 128)]
+PIECES = [(2, 24), (24, 80), (80, 128)]
+SCAL = [(2, 24), (24, 56), (104, 128)]
+VECT = [None, (56, 80), (80, 104)]
+CUT = 64
+DV = 16 * 24
+TB = W + DV
+MW, OW = 48, 34
 
 SCRATCH = {
     "dsc": ("dram", [8, 128, 128], "int32"),
+    "swap": ("dram", [2, 128, 128], "int32"),
     "land": ("sbuf", [128, 1024], "int32"),
     "parw": ("sbuf", [128, 128], "int32"),
     "tokc": ("sbuf", [128, 128], "int32"),
@@ -17,34 +23,32 @@ SCRATCH = {
     "acc": ("sbuf", [128, 128], "int32"),
     "tgt": ("sbuf", [128, 128], "int32"),
     "pcol": ("sbuf", [128, 1], "int32"),
-    "pa": ("sbuf", [128, 1], "int32"),
-    "pg": ("sbuf", [128, 1], "int32"),
+    "pi": ("sbuf", [128, 4], "int32"),
     "cst": ("sbuf", [128, 16], "float32"),
-    "mg": ("sbuf", [128, 128], "float32"),
+    "pair": ("sbuf", [128, 1], "bfloat16"),
+    "mg": ("sbuf", [128, 128], "bfloat16"),
     "strip": ("sbuf", [128, 144], "float32"),
-    "step": ("sbuf", [128, 32], "float32"),
-    "bm": ("sbuf", [128, 128], "float16"),
-    "bk2": ("sbuf", [128, 128], "float16"),
-    "em": ("sbuf", [128, 2048], "float16"),
+    "em": ("sbuf", [128, 1024], "float16"),
     "fm": ("sbuf", [128, 144], "bfloat16"),
     "fh": ("sbuf", [128, 144], "float16"),
-    "tokh": ("sbuf", [128, 128], "float16"),
-    "hiw": ("sbuf", [128, 128], "float16"),
+    "tok4": ("sbuf", [128, 4, 32], "float16"),
+    "tokt": ("sbuf", [128, 128], "float16"),
+    "hiw": ("sbuf", [128, 256], "float16"),
+    "mix": ("sbuf", [128, 256], "float16"),
     "lst": ("sbuf", [128, 128], "uint16"),
     "pars": ("sbuf", [128, 128], "float32"),
-    "ktmp": ("sbuf", [128, 2048], "float32"),
     "kk": ("sbuf", [128, 2048], "float32"),
     "eq": ("sbuf", [128, 2048], "bfloat16"),
     "offu": ("sbuf", [128, 128], "uint16"),
     "vals": ("sbuf", [128, 2048], "float32"),
-    "nxt": ("sbuf", [128, W + M], "float32"),
+    "nxt": ("sbuf", [128, TB + W + M], "float32"),
     "c16": ("sbuf", [128, 128], "bfloat16"),
     "arow": ("sbuf", [128, 128], "bfloat16"),
     "ones": ("sbuf", [128, 128], "bfloat16"),
     "mask": ("sbuf", [128, 32], "float32"),
-    "res": ("sbuf", [128, 16], "bfloat16"),
-    "md": ("sbuf", [128, 32 * D], "float16"),
-    "offw": ("sbuf", [128, 32 * D + 32], "uint16"),
+    "res": ("sbuf", [128, 48], "bfloat16"),
+    "md": ("sbuf", [128, MW * 2 * D], "float16"),
+    "offw": ("sbuf", [128, OW * 2 * D], "uint16"),
     "lu": ("sbuf", [128, 32], "uint16"),
     "lists": ("sbuf", [128, 32 * Q], "uint16"),
     "kvw": ("sbuf", [128, W * Q], "bfloat16"),
@@ -53,7 +57,7 @@ SCRATCH = {
     "psB": ("psum", [128, 2048], "float32"),
 }
 SEMAPHORES = ["vs", "ss", "ps", "gs", "ldD", "ldS", "ldM", "ldP", "ldO", "ldpar", "ldtok", "ldk0", "ldk1", "ldk2", "ldk3",
-              "sent", "aD", "aS", "aM", "aP", "lsent", "li0", "li1", "li2", "li3", "stored"]
+              "sent", "aD", "aS", "aM", "aP", "aX", "lsent", "stored", "li0", "li1", "li2", "li3"]
 
 
 def rank_program(g, core, T, topo):
@@ -105,124 +109,143 @@ def rank_program(g, core, T, topo):
     R = T.rank_of
 
     stage = lambda q, c, sem: q.dma_start(T.dsc[R(c)], piece(R(c))).then_inc(T.sem[sem], 16)
+    near = [c for grp in (plane, mate) for c in grp if topo.die(c) == topo.die(core)]
+    far = [c for grp in (plane, mate) for c in grp if topo.die(c) != topo.die(core)]
     for c in diag:
         stage(g.sync, c, "ldD")
-    for c in plane:
-        stage(g.sync, c, "ldS")
+    stage(g.sync, same[0], "ldP")
+    for c in near:
+        stage(g.sync, c, "ldM")
     g.sync.dma_start(slot(rank), piece(rank)).then_inc(T.sem.ldO, 16)
-    stage(g.scalar, same[0], "ldP")
-    g.scalar.dma_start(T.tokc[:], T.tok[:]).then_inc(T.sem.ldtok, 16)
+    for c in far:
+        stage(g.scalar, c, "ldS")
+    for u in range(2):
+        g.scalar.dma_start(T.tokc[:, 64 * u:64 * u + 64], T.tok[u::2, :]).then_inc(T.sem.ldtok, 16)
     g.scalar.dma_start(T.parw[:], T.par[:]).then_inc(T.sem.ldpar, 16)
-    for c in mate:
-        stage(g.scalar, c, "ldM")
 
     loose = dict(allow_small_or_imprecise_dtypes=True)
     i_p = done("g", g.iota(T.pcol[:], [[1, 1]], 0, 1))
-    i_mg = done("g", g.iota(T.mg[:], [[1, 8], [0, 16]], 0, 0, **loose))
+    i_mg = done("g", g.iota(T.mg[:], [[8, 8], [0, 16]], 0, 0, **loose))
     i_strip = done("g", g.iota(T.strip[:], [[1, 144]], 0, 0, **loose))
+    need("g", [("ldD", 32)])
+    g.remote_dma_fused([RemoteDMATransfer(dst_ids=[dst_id(c)], dma_engine_mask=bits(off[k * half:(k + 1) * half]),
+                                          remote_sem=T.sem.aD, src=T.dsc[R(c)], dst=slot(rank))
+                        for k, c in enumerate(diag)], local_sem=T.sem.sent)
+    need("g", [("ldS", 32)])
+    g.remote_dma_fused([RemoteDMATransfer(dst_ids=[dst_id(same[0])], dma_engine_mask=bits(inner[k * half:(k + 1) * half]),
+                                          remote_sem=T.sem.aX, src=T.dsc[R(c)], dst=T.swap[k])
+                        for k, c in enumerate(far)], local_sem=T.sem.sent)
     need("g", [("ldP", 16)])
     g.remote_dma_fused([RemoteDMATransfer(dst_ids=[dst_id(same[0])], dma_engine_mask=bits(inner),
                                           remote_sem=T.sem.aP, src=T.dsc[R(same[0])], dst=slot(rank))],
                        local_sem=T.sem.sent)
-    for grp, ld, ar in ((diag, "ldD", "aD"), (plane, "ldS", "aS"), (mate, "ldM", "aM")):
-        need("g", [(ld, 32)])
-        g.remote_dma_fused([RemoteDMATransfer(dst_ids=[dst_id(c)], dma_engine_mask=bits(off[k * half:(k + 1) * half]),
-                                              remote_sem=T.sem[ar], src=T.dsc[R(c)], dst=slot(rank))
-                            for k, c in enumerate(grp)], local_sem=T.sem.sent)
-    done("g", g.iota(T.c16[:], [[16, 128]], W, 0, **loose))
+    need("g", [("ldM", 32), ("aX", len(inner))])
+    for k, (c, ar) in enumerate(zip(near, ("aS", "aM"))):
+        g.remote_dma_fused([RemoteDMATransfer(dst_ids=[dst_id(c)], dma_engine_mask=bits(off), remote_sem=T.sem[ar],
+                                              srcs=[T.dsc[R(c)], T.swap[k]], dsts=[slot(rank)], alu_op=2)],
+                           local_sem=T.sem.sent)
+    for ca, cb in (VECT[1], VECT[2]):
+        done("g", g.iota(T.c16[:, ca:cb], [[16, cb - ca]], W, 0, **loose))
+    for ca, cb in ((SCAL[0][0], SCAL[1][1]), SCAL[2]):
+        done("g", g.iota(T.c16[:, ca:cb], [[16, cb - ca]], W, 0, **loose))
     i_ar = done("g", g.iota(T.arow[:], [[0, 8], [1, 16]], 0, 0, **loose))
-    i_val = []
-    for n, (ca, cb) in enumerate(PIECES):
-        j = 16 * ca if n else 0
-        i_val.append(done("g", g.iota(T.vals[:, j:16 * cb], [[1, 16 * cb - j]], 1 + j, 0, **loose)))
-    i_step = done("g", g.iota(T.step[:], [[0, 2], [1, 16]], 0, 0, **loose))
+    i_val = {}
+    for ca, cb in (SCAL[0], SCAL[1], VECT[1], VECT[2], SCAL[2]):
+        i_val[ca] = done("g", g.iota(T.vals[:, 16 * ca:16 * cb], [[1, 16 * (cb - ca)]], 1 + 16 * ca, 0, **loose))
 
     me = rank // 2
     heads = [c for c in diag + plane + mate if R(c) % 2 == rank % 2]
     order = [None] + [c for c in mate + plane + diag if c in heads]
     member = lambda c: me if c is None else R(c) // 2
-    need("y", [("sent", 6 * half + len(inner))])
+    need("y", [("sent", 3 * len(off) + 2 * len(inner))])
     for c in order:
         i = member(c)
         g.sync.dma_start(T.kvw[:, i * W + Z:(i + 1) * W], T.kv[:, i * M:(i + 1) * M]).then_inc(T.sem["ldk%d" % i], 16)
 
     v, t, s = g.vector, g.tensor, g.scalar
     col = lambda k: T.cst[:, k:k + 1]
+    icol = lambda k: T.pi[:, k:k + 1]
 
+    ZW = 256
+    v_z = done("v", v.memset(T.nxt[:, TB:TB + ZW], 0.0))
     need("v", [i_p])
-    b = done("v", v.tensor_scalar(T.pg[:], T.pcol[:], 4, None, A.arith_shift_right))
-    a = done("v", v.tensor_scalar(T.pa[:], T.pcol[:], 15, None, A.bitwise_and))
-    need("v", [b])
-    c0 = done("v", v.tensor_copy(col(2), T.pg[:]))
-    need("v", [a])
-    done("v", v.tensor_scalar(col(1), T.pa[:], 1.0, None, A.add))
-    done("v", v.tensor_copy(col(0), T.pa[:]))
+    ph = done("v", v.tensor_scalar(icol(0), T.pcol[:], 1, None, A.arith_shift_right))
+    po = done("v", v.tensor_scalar(icol(1), T.pcol[:], 1, None, A.bitwise_and))
+    pa = done("v", v.tensor_scalar(icol(2), T.pcol[:], 15, None, A.bitwise_and))
+    pg = done("v", v.tensor_scalar(icol(3), T.pcol[:], 112, None, A.bitwise_and))
+    need("v", [ph])
+    c0 = done("v", v.tensor_copy(T.pair[:], icol(0)))
+    need("v", [po])
+    done("v", v.tensor_scalar(col(1), icol(1), 32.0, -32.0, A.mult, A.add))
+    done("v", v.tensor_scalar(col(2), icol(1), 6144.0, -2048.0, A.mult, A.add))
     need("v", [c0, i_mg])
-    x = done("v", v.tensor_scalar(T.bm[:], T.mg[:], col(2), None, A.is_equal))
-    need("v", [x])
-    x = done("v", v.tensor_scalar(T.bk2[:], T.bm[:], col(1), None, A.mult))
-    kb = done("v", v.tensor_scalar(col(3), col(0), -4096.0, 2048.0, A.mult, A.add))
-    done("v", v.memset(T.res[:], 1.0))
-    need("v", [x])
-    for k in range(16):
-        done("v", v.tensor_scalar(T.em[:, blk(k)], T.bk2[:], float(k + 1), None, A.is_equal))
-    need("v", [("ldtok", 16)])
-    v_tok = done("v", v.tensor_scalar(T.tokh[:], T.tokc[:], -2048.0, None, A.add))
+    for q in range(8):
+        done("v", v.tensor_scalar(T.em[:, blk(q)], T.mg[:], float(q), T.pair[:], A.add, A.is_equal))
+    need("v", [pg])
+    done("v", v.tensor_scalar(col(3), icol(1), -32.0, None, A.mult))
+    done("v", v.tensor_scalar(col(4), icol(1), -6144.0, 4096.0, A.mult, A.add))
+    kb = done("v", v.tensor_scalar(col(5), icol(2), 4096.0, 4096.0, A.mult, A.add))
+    done("v", v.tensor_scalar(col(6), icol(3), 15.0, None, A.add))
+
+    need("v", [("ldtok", 32)])
+    for u in range(2):
+        for e in range(2):
+            x = done("v", v.tensor_scalar(T.tok4[:, :, 16 * u + 1 - e:16 * u + 16:2], T.tokc[:, 64 * u + e:64 * u + 64:2],
+                                          -2048.0, None, A.add))
     need("v", [("ldpar", 16)])
     x1 = done("v", v.tensor_scalar(T.it1[:], T.parw[:], 1920, None, A.bitwise_and))
-    x2 = done("v", v.tensor_scalar(T.it2[:], T.parw[:], 127, None, A.bitwise_and))
+    need("v", [x])
+    for b in range(4):
+        done("v", v.transpose(T.tokt[:, 32 * b:32 * b + 32], T.tok4[:, b, :]))
+    v_mix = []
     need("v", [x1])
-    v_hi = done("v", v.tensor_scalar(T.hiw[:], T.it1[:], 32.0, None, A.mult))
-    need("v", [x2])
-    done("v", v.tensor_copy(T.lst[:], T.it2[:]))
+    hs = [done("v", v.tensor_scalar(T.hiw[:, blk(e)], T.it1[:], col(1 + 2 * e), col(2 + 2 * e), A.mult, A.add)) for e in range(2)]
+    for e in range(2):
+        need("v", [hs[e]])
+        for b in range(4):
+            cs = slice(128 * e + b, 128 * e + 128, 4)
+            x = done("v", v.tensor_tensor(T.mix[:, cs], T.tokt[:, 32 * b:32 * b + 32], T.hiw[:, cs], A.min))
+        v_mix.append(x)
+    x2 = done("v", v.tensor_scalar(T.it2[:], T.parw[:], 127, None, A.bitwise_and))
     done("v", v.tensor_scalar(T.pars[:], T.parw[:], 1.0, None, A.add))
-    c5 = done("v", v.tensor_scalar(col(5), col(2), 16.0, 15.0, A.mult, A.add))
+    need("v", [x2, i_strip])
+    done("v", v.tensor_copy(T.lst[:], T.it2[:]))
     v_ones = done("v", v.memset(T.ones[:], 1.0 / 128))
-    need("v", [c5, i_strip])
-    v_f = done("v", v.tensor_scalar(T.fm[:], T.strip[:], col(5), -8192.0, A.is_equal, A.mult))
-    v_fh = done("v", v.tensor_scalar(T.fh[:], T.strip[:], col(5), None, A.is_equal))
-    lcol = lambda d, h: 32 * d + 16 * h + 16
-    last = [done("v", v.tensor_scalar(T.offw[:, lcol(0, h):lcol(0, h) + 1], col(0), float(1 + 16 * h), None, A.add))
-            for h in range(2)]
+    v_f = done("v", v.tensor_scalar(T.fm[:], T.strip[:], col(6), -8192.0, A.is_equal, A.mult))
+    v_fh = done("v", v.tensor_scalar(T.fh[:], T.strip[:], col(6), None, A.is_equal))
+
+    ks = [2 * q + e for e in range(2) for q in range(8)]
+    pk = []
+    for n, k in enumerate(ks):
+        need("p", [v_mix[k % 2]])
+        ins = t.matmul(T.psB[:, blk(n)], T.em[:, blk(k // 2)], T.mix[:, blk(k % 2)], True, True)
+        if n % 4 == 3:
+            pk.append(done("p", ins))
+
+    zeros = lambda n: T.nxt[:, TB:TB + n]
+    need("s", [v_z])
+    done("s", s.activation(T.nxt[:, TB + M:TB + W], zeros(Z), AF.Silu, scale=0.0))
+    for j in range(TB + ZW, TB + M, ZW):
+        x = done("s", s.activation(T.nxt[:, j:j + ZW], zeros(ZW), AF.Identity))
+
+    def kout(q, bank):
+        need(q, [pk[bank], kb])
+        for n in range(4 * bank, 4 * bank + 4):
+            o, i = T.kk[:, ks[n]::16], T.psB[:, blk(n)]
+            e = done(q, s.activation(o, i, AF.Identity, bias=col(5), scale=1.0) if q == "s"
+                     else v.tensor_scalar(o, i, col(5), None, A.add))
+        return e
+
+    for bank in (0, 2, 3):
+        s_k = kout("s", bank)
+    need("s", [x])
+    done("s", s.activation(T.nxt[:, 0:M], zeros(M), AF.Identity))
+    done("s", s.activation(T.nxt[:, M:TB], zeros(TB - M), AF.Identity))
     for i in range(Q):
-        done("v", v.memset(T.kvw[:, i * W:i * W + Z], 0.0))
+        s_zero = done("s", s.activation(T.kvw[:, i * W:i * W + Z], zeros(Z), AF.Identity))
+    v_k = kout("v", 1)
 
-    pa_done, pb_done = [], []
-    for hf in range(2):
-        need("p", [v_tok])
-        for bank in (2 * hf, 2 * hf + 1):
-            for k in range(4 * bank, 4 * bank + 4):
-                ins = t.matmul(T.psA[:, blk(k)], T.em[:, blk(k)], T.tokh[:], True, True)
-            pa_done.append(done("p", ins))
-        need("p", [v_hi])
-        for bank in range(2):
-            for k in range(8 * bank, 8 * bank + 8):
-                o = H * hf + 64 * k
-                ins = t.matmul(T.psB[:, o:o + 64], T.em[:, blk(k)], T.hiw[:, 64 * hf:64 * hf + 64], True, True)
-            pb_done.append(done("p", ins))
-
-    need("s", [i_mg])
-    done("s", s.activation(T.nxt[:, M:W], T.mg[:, 0:Z], AF.Silu, scale=0.0))
-    ks = []
-    for bank in range(4):
-        need("s", [pa_done[bank], kb])
-        cs = slice(bank * 512, (bank + 1) * 512)
-        ks.append(done("s", s.activation(T.ktmp[:, cs], T.psA[:, cs], AF.Identity, bias=col(3), scale=1.0)))
-    need("s", ks)
-    s_zero = done("s", s.activation(T.nxt[:, 0:M], T.ktmp[:], AF.Identity, scale=0.0))
-
-    def ksum(hf):
-        out = []
-        need("v", [ks[2 * hf], ks[2 * hf + 1]])
-        for k in range(16):
-            need("v", [pb_done[2 * hf + k // 8]])
-            o, js = H * hf + 64 * k, slice(H * hf + k, H * hf + H, 16)
-            out.append(done("v", v.tensor_tensor(T.kk[:, js], T.psB[:, o:o + 64], T.ktmp[:, js], A.add)))
-        return out
-
-    v_kA = ksum(0)
-
-    need("p", [v_ones, v_f, i_ar] + ks)
+    need("p", [v_ones, v_f, i_ar])
     for n, (ca, cb) in enumerate(PIECES):
         ps = T.psA[:, n * 512:n * 512 + cb - ca]
         t.matmul(ps, T.ones[:], T.c16[:, ca:cb], True, False)
@@ -238,87 +261,118 @@ def rank_program(g, core, T, topo):
     def top(o, p, q, deps=((), ())):
         return both(lambda c: v.tensor_tensor(o(c), p(c), q(c), A.max), deps)
 
+    mdc = lambda d, h: MW * (2 * d + h)
+    lcol = lambda d, h: OW * (2 * d + h) + 32
+    last, v_m0 = [], []
+
+    def walk_tiles():
+        x = done("v", v.tensor_copy(col(7), icol(2)))
+        ys = [done("v", v.tensor_scalar(col(8 + h), icol(2), float(1 + 16 * h), None, A.add)) for h in range(2)]
+        done("v", v.memset(T.res[:], 1.0))
+        done("v", v.tensor_scalar(T.md[:, 32::MW], T.strip[:, 0:2 * D], 0.0, float(TB), A.mult, A.add))
+        need("v", [x])
+        for h in range(2):
+            x = done("v", v.tensor_scalar(T.mask[:, 16 * h:16 * h + 16], T.strip[:, 0:16], col(7), None, A.is_equal))
+        need("v", ys)
+        for h in range(2):
+            b = lcol(0, h)
+            last.append(done("v", v.tensor_scalar(T.offw[:, b:b + 2], T.strip[:, 0:2], float(TB), col(8 + h), A.mult, A.add)))
+        need("v", [x])
+        v_m0.append(done("v", v.tensor_tensor(T.md[:, 0:32], T.mask[:], T.strip[:, 1:33], A.mult)))
+
     part = lambda r: (lambda c: T.land[:, r * 128 + c.start:r * 128 + c.stop])
-    acc, full = (lambda c: T.psB[:, 512 + c.start:512 + c.stop]), (lambda c: T.acc[:, c])
-    need("v", [v_kA[9], ("ldO", 16), ("aP", len(inner))])
+    acc, full = (lambda c: T.psA[:, 1536 + c.start:1536 + c.stop]), (lambda c: T.acc[:, c])
+    need("v", [("ldO", 16), ("aP", len(inner))])
     x = top(acc, part(rank), part(R(same[0])))
-    for grp, ar in ((diag, "aD"), (plane, "aS"), (mate, "aM")):
-        if grp is plane:
-            v_k = ksum(1)[-1]
-        need("v", [(ar, 2 * half)])
+    for grp, ar in ((diag, "aD"), (near[:1], "aS"), (near[1:], "aM")):
+        if ar == "aS":
+            walk_tiles()
+        need("v", [(ar, len(off))])
         for c in grp:
-            x = top(full if c == mate[-1] else acc, acc, part(R(c)), x)
+            x = top(full if c == near[-1] else acc, acc, part(R(c)), x)
     x = both(lambda c: v.tensor_scalar(T.tgt[:, c], T.acc[:, c], 4095, None, A.bitwise_and), x)
-    need("v", x[1] + [v_k])
+    need("v", x[1] + [s_k])
 
-    p_ok = []
+    p_ok, placed = [], []
 
-    def fit(n):
+    def fit(ca, cb):
+        return done("v", v.tensor_tensor(T.eq[:, 16 * ca:16 * cb], T.tgt[:].indirect(T.lst[:, ca:cb]), T.kk[:, 16 * ca:16 * cb], A.is_equal))
+
+    def fold(n, e):
         ca, cb = PIECES[n]
-        e = done("v", v.tensor_tensor(T.eq[:, 16 * ca:16 * cb], T.tgt[:].indirect(T.lst[:, ca:cb]), T.kk[:, 16 * ca:16 * cb], A.is_equal))
         need("p", [e])
         for k in range(16):
             ins = t.matmul(T.psA[:, n * 512:n * 512 + cb - ca], T.fm[:, 15 - k:143 - k], T.eq[:, 16 * ca + k:16 * cb:16], False, k == 15)
         p_ok.append(done("p", ins))
 
-    scat = [s_zero]
+    scat = {"s": s_zero, "v": s_zero}
+
+    def scatter(q, n):
+        ca, cb = (SCAL if q == "s" else VECT)[n]
+        need(q, [placed[n], i_val[ca], scat[q]])
+        src, o = T.vals[:, 16 * ca:16 * cb], T.offu[:, ca:cb]
+        scat[q] = done(q, s.activation(T.nxt[:, TB:TB + W + M].indirect(o), src, AF.Silu) if q == "s"
+                       else v.tensor_copy(T.nxt[:, 0:TB].indirect(o), src))
 
     def place(n):
         ca, cb = PIECES[n]
         need("v", [p_ok[n]])
-        o = done("v", v.tensor_tensor(T.offu[:, ca:cb], T.psA[:, n * 512:n * 512 + cb - ca], T.pars[:, ca:cb], A.max))
-        need("s", [o, i_val[n], scat[-1]])
-        scat.append(done("s", s.activation(T.nxt[:].indirect(T.offu[:, ca:cb]), T.vals[:, 16 * ca:16 * cb], AF.Silu)))
+        placed.append(done("v", v.tensor_tensor(T.offu[:, ca:cb], T.psA[:, n * 512:n * 512 + cb - ca], T.pars[:, ca:cb], A.max)))
+        scatter("s", n)
 
-    fit(0)
-    for n in range(1, len(PIECES)):
-        fit(n)
-        place(n - 1)
-    place(len(PIECES) - 1)
+    fold(0, fit(*PIECES[0]))
+    fit(PIECES[1][0], CUT)
+    place(0)
+    fold(1, fit(CUT, PIECES[1][1]))
+    fold(2, fit(*PIECES[2]))
+    place(1)
+    scatter("v", 1)
+    place(2)
+    scatter("v", 2)
 
-    need("v", [i_step])
-    x = done("v", v.tensor_scalar(T.mask[:], T.step[:], col(0), None, A.is_equal))
-    need("v", [x])
-    v_m0 = done("v", v.tensor_tensor(T.md[:, 0:32], T.mask[:], T.vals[:, 0:32], A.mult))
+    def collect(d, h, dep):
+        need("p", [dep])
+        for u in range(2):
+            b = mdc(d, h) + 16 * u
+            end = d == D - 1 and h == 1 and u == 1
+            ins = t.matmul(T.psB[:, 16 * h:16 * h + 16], T.fh[:, 15 - d:143 - d], T.md[:, b:b + 16], False, end)
+        return done("p", ins) if end else None
 
-    def collect(d, dep):
-        need("p", [dep, v_fh, v_k])
-        ins = t.matmul(T.psB[:, 0:32], T.fh[:, 15 - d:143 - d], T.md[:, 32 * d:32 * d + 32], d == 0, d == D - 1)
-        return done("p", ins) if d == D - 1 else None
+    def keys(q, c, sa, sb, dep):
+        i = member(c)
+        need(q, [("ldk%d" % i, 16), dep] + ([("li%d" % i, len(off))] if c is not None else []))
+        src, b = (T.lu, 0) if c is None else (T.lists, S * i)
+        win = T.kvw[:, i * W:(i + 1) * W].indirect(src[:, b + sa:b + sb])
+        o = T.ysb[:, D * (S * i + sa):D * (S * i + sb)]
+        return done(q, s.activation(o, win, AF.Copy) if q == "s" else v.tensor_copy(o, win))
 
-    collect(0, v_m0)
-    need("v", [scat[-1]])
+    need("p", [v_m0[0], v_fh, v_k, s_k])
+    t.matmul(T.psB[:, 0:32], T.fh[:, 15:143], T.md[:, 0:32], True, False)
+    need("v", [scat["s"], scat["v"]])
     for d in range(1, D):
         xs = []
         for h in range(2):
             need("v", [last[h]])
-            b = lcol(d - 1, h)
-            xs.append(done("v", v.tensor_tensor(T.md[:, 32 * d + 16 * h:32 * d + 16 * h + 16],
-                                                T.nxt[:, 0:W].indirect(T.offw[:, b:b + 1]), T.mask[:, 0:16], A.mult)))
-        p_l = collect(d, xs[1])
+            b, m = lcol(d - 1, h), mdc(d, h)
+            xs.append(done("v", v.tensor_tensor(T.md[:, m:m + 32], T.nxt[:, 0:TB + W].indirect(T.offw[:, b:b + 2]), T.mask[:], A.mult)))
+            p_l = collect(d, h, xs[h])
         if d < D - 1:
             for h in range(2):
                 need("v", [xs[h]])
-                b = lcol(d, h)
-                last[h] = done("v", v.tensor_tensor_scan(T.offw[:, b - 15:b + 1], T.res[:],
-                                                         T.md[:, 32 * d + 16 * h:32 * d + 16 * h + 16], 0.0, A.mult, A.add))
+                b, m = lcol(d, h), mdc(d, h)
+                last[h] = done("v", v.tensor_tensor_scan(T.offw[:, b - 31:b + 2], T.res[:, 0:33], T.md[:, m:m + 33], 0.0, A.mult, A.add))
     need("v", [p_l])
     v_lu = done("v", v.tensor_scalar(T.lu[:], T.psB[:, 0:32], float(Z - 1), None, A.add))
 
     need("g", [v_lu])
-    mine = T.lists[:, me * 32:(me + 1) * 32]
+    mine = T.lists[:, me * S:(me + 1) * S]
     g.remote_dma_fused([RemoteDMATransfer(dst_ids=[dst_id(c) for c in heads], dma_engine_mask=bits(off), remote_sem=T.sem["li%d" % me],
                                           srcs=[T.lu[:]], dsts=[mine for c in heads], alu_op=0)], local_sem=T.sem.lsent)
 
     for c in order:
         i = member(c)
-        win = T.kvw[:, i * W:(i + 1) * W]
-        src = T.lu if c is None else T.lists
-        b0 = 0 if c is None else 32 * i
-        for q in "vs":
-            need(q, [("ldk%d" % i, 16), v_lu] + ([("li%d" % i, len(off))] if c is not None else []))
-        e1 = done("v", v.tensor_copy(T.ysb[:, i * 512:i * 512 + 256], win.indirect(src[:, b0:b0 + 16])))
-        e2 = done("s", s.activation(T.ysb[:, i * 512 + 256:(i + 1) * 512], win.indirect(src[:, b0 + 16:b0 + 32]), AF.Copy))
+        e1 = keys("v", c, 0, S // 2, v_lu)
+        e2 = keys("s", c, S // 2, S, v_lu)
         need("y", [e1, e2])
         g.sync.dma_start(T.y[:, i * 512:(i + 1) * 512], T.ysb[:, i * 512:(i + 1) * 512]).then_inc(T.sem.stored, 16)
     need("g", [("lsent", len(off)), ("gs", count["g"]), ("ps", count["p"])])

@@ -4,17 +4,21 @@ from concourse.mybir import AluOpType as A, ActivationFunctionType as AF
 M, S, D, Q = 2048, 32, 16, 4
 Z = 16
 W = M + Z
-PIECES = [(2, 24), (24, 80), (80, 128)]
-SCAL = [(2, 24), (24, 56), (104, 128)]
-VECT = [None, (56, 80), (80, 104)]
-CUT = 64
-DV = 16 * 24
+PIECES = [(58, 72), (2, 58), (72, 128)]
+OWN = (34, 96)
+LENT = [(2, 34), (96, 128)]
+SCAL = [(58, 72), (2, 30), (100, 128)]
+VECT = [None, (30, 58), (72, 100)]
+DV = 16 * 28
 TB = W + DV
+EARLY = 13
+LATE = [D - 1] + list(range(EARLY, D - 1))
+NL = 2 * len(LATE)
 MW, OW = 48, 34
 
 SCRATCH = {
     "dsc": ("dram", [8, 128, 128], "int32"),
-    "swap": ("dram", [2, 128, 128], "int32"),
+    "swap": ("dram", [128, 128], "int32"),
     "land": ("sbuf", [128, 1024], "int32"),
     "parw": ("sbuf", [128, 128], "int32"),
     "tokc": ("sbuf", [128, 128], "int32"),
@@ -51,13 +55,15 @@ SCRATCH = {
     "offw": ("sbuf", [128, OW * 2 * D], "uint16"),
     "lu": ("sbuf", [128, 32], "uint16"),
     "lists": ("sbuf", [128, 32 * Q], "uint16"),
+    "tail": ("sbuf", [128, 80], "uint16"),
+    "tails": ("sbuf", [128, 16 * Q], "uint16"),
     "kvw": ("sbuf", [128, W * Q], "bfloat16"),
     "ysb": ("sbuf", [128, 512 * Q], "bfloat16"),
     "psA": ("psum", [128, 2048], "float32"),
     "psB": ("psum", [128, 2048], "float32"),
 }
-SEMAPHORES = ["vs", "ss", "ps", "gs", "ldD", "ldS", "ldM", "ldP", "ldO", "ldpar", "ldtok", "ldk0", "ldk1", "ldk2", "ldk3",
-              "sent", "aD", "aS", "aM", "aP", "aX", "lsent", "stored", "li0", "li1", "li2", "li3"]
+SEMAPHORES = ["vs", "ss", "ps", "gs", "ldD", "ldX", "ldS", "ldM", "ldP", "ldO", "ldpar", "ldtok", "ldk0", "ldk1", "ldk2", "ldk3",
+              "sent", "aD", "aS", "aM", "aP", "aX", "lsent", "stored", "li0", "li1", "li2", "li3", "lj0", "lj1", "lj2", "lj3"]
 
 
 def rank_program(g, core, T, topo):
@@ -109,16 +115,17 @@ def rank_program(g, core, T, topo):
     R = T.rank_of
 
     stage = lambda q, c, sem: q.dma_start(T.dsc[R(c)], piece(R(c))).then_inc(T.sem[sem], 16)
-    near = [c for grp in (plane, mate) for c in grp if topo.die(c) == topo.die(core)]
-    far = [c for grp in (plane, mate) for c in grp if topo.die(c) != topo.die(core)]
-    for c in diag:
-        stage(g.sync, c, "ldD")
+    ondie = lambda grp, yes: [c for c in grp if (topo.die(c) == topo.die(core)) == yes][0]
+    near, far = ondie(diag, True), ondie(diag, False)
+    first, second = ([ondie(plane, yes), ondie(mate, yes)] for yes in (False, True))
+    stage(g.sync, first[0], "ldD")
+    stage(g.scalar, first[1], "ldD")
+    stage(g.sync, far, "ldX")
+    for c in second:
+        stage(g.sync, c, "ldS")
+    stage(g.sync, near, "ldM")
     stage(g.sync, same[0], "ldP")
-    for c in near:
-        stage(g.sync, c, "ldM")
     g.sync.dma_start(slot(rank), piece(rank)).then_inc(T.sem.ldO, 16)
-    for c in far:
-        stage(g.scalar, c, "ldS")
     for u in range(2):
         g.scalar.dma_start(T.tokc[:, 64 * u:64 * u + 64], T.tok[u::2, :]).then_inc(T.sem.ldtok, 16)
     g.scalar.dma_start(T.parw[:], T.par[:]).then_inc(T.sem.ldpar, 16)
@@ -127,26 +134,23 @@ def rank_program(g, core, T, topo):
     i_p = done("g", g.iota(T.pcol[:], [[1, 1]], 0, 1))
     i_mg = done("g", g.iota(T.mg[:], [[8, 8], [0, 16]], 0, 0, **loose))
     i_strip = done("g", g.iota(T.strip[:], [[1, 144]], 0, 0, **loose))
+    def send(moves):
+        g.remote_dma_fused([RemoteDMATransfer(dst_ids=[dst_id(c)], dma_engine_mask=bits(es), remote_sem=T.sem[ar], srcs=srcs,
+                                              dsts=[dst], alu_op=2 if len(srcs) > 1 else 0)
+                            for c, es, ar, srcs, dst in moves], local_sem=T.sem.sent)
+
+    pair = lambda grp, ar: [(c, off[k * half:(k + 1) * half], ar, [T.dsc[R(c)]], slot(rank)) for k, c in enumerate(grp)]
     need("g", [("ldD", 32)])
-    g.remote_dma_fused([RemoteDMATransfer(dst_ids=[dst_id(c)], dma_engine_mask=bits(off[k * half:(k + 1) * half]),
-                                          remote_sem=T.sem.aD, src=T.dsc[R(c)], dst=slot(rank))
-                        for k, c in enumerate(diag)], local_sem=T.sem.sent)
+    send(pair(first, "aD"))
+    need("g", [("ldX", 16)])
+    send([(same[0], inner, "aX", [T.dsc[R(far)]], T.swap[:])])
     need("g", [("ldS", 32)])
-    g.remote_dma_fused([RemoteDMATransfer(dst_ids=[dst_id(same[0])], dma_engine_mask=bits(inner[k * half:(k + 1) * half]),
-                                          remote_sem=T.sem.aX, src=T.dsc[R(c)], dst=T.swap[k])
-                        for k, c in enumerate(far)], local_sem=T.sem.sent)
+    send(pair(second, "aS"))
     need("g", [("ldP", 16)])
-    g.remote_dma_fused([RemoteDMATransfer(dst_ids=[dst_id(same[0])], dma_engine_mask=bits(inner),
-                                          remote_sem=T.sem.aP, src=T.dsc[R(same[0])], dst=slot(rank))],
-                       local_sem=T.sem.sent)
-    need("g", [("ldM", 32), ("aX", len(inner))])
-    for k, (c, ar) in enumerate(zip(near, ("aS", "aM"))):
-        g.remote_dma_fused([RemoteDMATransfer(dst_ids=[dst_id(c)], dma_engine_mask=bits(off), remote_sem=T.sem[ar],
-                                              srcs=[T.dsc[R(c)], T.swap[k]], dsts=[slot(rank)], alu_op=2)],
-                           local_sem=T.sem.sent)
-    for ca, cb in (VECT[1], VECT[2]):
-        done("g", g.iota(T.c16[:, ca:cb], [[16, cb - ca]], W, 0, **loose))
-    for ca, cb in ((SCAL[0][0], SCAL[1][1]), SCAL[2]):
+    send([(same[0], inner, "aP", [T.dsc[R(same[0])]], slot(rank))])
+    need("g", [("ldM", 16), ("aX", len(inner))])
+    send([(near, off, "aM", [T.dsc[R(near)], T.swap[:]], slot(rank))])
+    for ca, cb in SCAL + VECT[1:]:
         done("g", g.iota(T.c16[:, ca:cb], [[16, cb - ca]], W, 0, **loose))
     i_ar = done("g", g.iota(T.arow[:], [[0, 8], [1, 16]], 0, 0, **loose))
     i_val = {}
@@ -154,8 +158,8 @@ def rank_program(g, core, T, topo):
         i_val[ca] = done("g", g.iota(T.vals[:, 16 * ca:16 * cb], [[1, 16 * (cb - ca)]], 1 + 16 * ca, 0, **loose))
 
     me = rank // 2
-    heads = [c for c in diag + plane + mate if R(c) % 2 == rank % 2]
-    order = [None] + [c for c in mate + plane + diag if c in heads]
+    heads = [c for c in diag + mate + plane if R(c) % 2 == rank % 2]
+    order = [None] + [c for c in mate + diag + plane if c in heads]
     member = lambda c: me if c is None else R(c) // 2
     need("y", [("sent", 3 * len(off) + 2 * len(inner))])
     for c in order:
@@ -166,7 +170,7 @@ def rank_program(g, core, T, topo):
     col = lambda k: T.cst[:, k:k + 1]
     icol = lambda k: T.pi[:, k:k + 1]
 
-    ZW = 256
+    ZW, ZV = 256, 896
     v_z = done("v", v.memset(T.nxt[:, TB:TB + ZW], 0.0))
     need("v", [i_p])
     ph = done("v", v.tensor_scalar(icol(0), T.pcol[:], 1, None, A.arith_shift_right))
@@ -186,6 +190,8 @@ def rank_program(g, core, T, topo):
     done("v", v.tensor_scalar(col(4), icol(1), -6144.0, 4096.0, A.mult, A.add))
     kb = done("v", v.tensor_scalar(col(5), icol(2), 4096.0, 4096.0, A.mult, A.add))
     done("v", v.tensor_scalar(col(6), icol(3), 15.0, None, A.add))
+    done("v", v.tensor_scalar(col(10), icol(2), -4096.0, -4096.0, A.mult, A.add))
+    done("v", v.memset(T.nxt[:, 0:ZW], 0.0))
 
     need("v", [("ldtok", 32)])
     for u in range(2):
@@ -215,41 +221,37 @@ def rank_program(g, core, T, topo):
     v_fh = done("v", v.tensor_scalar(T.fh[:], T.strip[:], col(6), None, A.is_equal))
 
     ks = [2 * q + e for e in range(2) for q in range(8)]
+    va, vb = OWN
+    kps = lambda n: T.psB[:, 64 * n:64 * n + vb - va]
+    kept = lambda n: slice(512 * (2 + n), 512 * (3 + n))
+    mix = lambda k, ca, cb: T.mix[:, 128 * (k % 2) + ca:128 * (k % 2) + cb]
     pk = []
     for n, k in enumerate(ks):
         need("p", [v_mix[k % 2]])
-        ins = t.matmul(T.psB[:, blk(n)], T.em[:, blk(k // 2)], T.mix[:, blk(k % 2)], True, True)
-        if n % 4 == 3:
+        ins = t.matmul(kps(n), T.em[:, blk(k // 2)], mix(k, va, vb), True, True)
+        if n % 8 == 7:
             pk.append(done("p", ins))
+    for n, (ca, cb) in enumerate(LENT):
+        for k in ks:
+            ins = t.matmul(T.psB[:, kept(n).start + k:kept(n).stop:16], T.em[:, blk(k // 2)], mix(k, ca, cb), True, True)
+        pk.append(done("p", ins))
+    need("p", [v_f, i_ar])
+    for n, (ca, cb) in enumerate(PIECES):
+        ps = T.psA[:, n * 512:n * 512 + cb - ca]
+        t.matmul(ps, T.ones[:], T.c16[:, ca:cb], True, False)
+        t.matmul(ps, T.arow[:], T.ones[:, 0:cb - ca], False, False)
 
     zeros = lambda n: T.nxt[:, TB:TB + n]
     need("s", [v_z])
     done("s", s.activation(T.nxt[:, TB + M:TB + W], zeros(Z), AF.Silu, scale=0.0))
     for j in range(TB + ZW, TB + M, ZW):
         x = done("s", s.activation(T.nxt[:, j:j + ZW], zeros(ZW), AF.Identity))
-
-    def kout(q, bank):
-        need(q, [pk[bank], kb])
-        for n in range(4 * bank, 4 * bank + 4):
-            o, i = T.kk[:, ks[n]::16], T.psB[:, blk(n)]
-            e = done(q, s.activation(o, i, AF.Identity, bias=col(5), scale=1.0) if q == "s"
-                     else v.tensor_scalar(o, i, col(5), None, A.add))
-        return e
-
-    for bank in (0, 2, 3):
-        s_k = kout("s", bank)
+    done("s", s.activation(T.nxt[:, ZV:ZV + ZW], zeros(ZW), AF.Identity))
+    for n, k in enumerate(ks):
+        need("s", [pk[n // 8], kb])
+        s_k = done("s", s.activation(T.kk[:, 16 * va + k:16 * vb:16], kps(n), AF.Identity, bias=col(5), scale=1.0))
     need("s", [x])
-    done("s", s.activation(T.nxt[:, 0:M], zeros(M), AF.Identity))
-    done("s", s.activation(T.nxt[:, M:TB], zeros(TB - M), AF.Identity))
-    for i in range(Q):
-        s_zero = done("s", s.activation(T.kvw[:, i * W:i * W + Z], zeros(Z), AF.Identity))
-    v_k = kout("v", 1)
-
-    need("p", [v_ones, v_f, i_ar])
-    for n, (ca, cb) in enumerate(PIECES):
-        ps = T.psA[:, n * 512:n * 512 + cb - ca]
-        t.matmul(ps, T.ones[:], T.c16[:, ca:cb], True, False)
-        t.matmul(ps, T.arow[:], T.ones[:, 0:cb - ca], False, False)
+    s_zero = done("s", s.activation(T.nxt[:, ZV + ZW:TB], zeros(TB - ZV - ZW), AF.Identity))
 
     def both(op, deps=((), ())):
         out = []
@@ -282,14 +284,15 @@ def rank_program(g, core, T, topo):
 
     part = lambda r: (lambda c: T.land[:, r * 128 + c.start:r * 128 + c.stop])
     acc, full = (lambda c: T.psA[:, 1536 + c.start:1536 + c.stop]), (lambda c: T.acc[:, c])
-    need("v", [("ldO", 16), ("aP", len(inner))])
-    x = top(acc, part(rank), part(R(same[0])))
-    for grp, ar in ((diag, "aD"), (near[:1], "aS"), (near[1:], "aM")):
-        if ar == "aS":
-            walk_tiles()
+    walk_tiles()
+    need("v", [("ldO", 16), ("aD", len(off))])
+    x = top(acc, part(rank), part(R(first[0])))
+    for grp, ar in ((first[1:], "aD"), (same, "aP"), (second, "aS"), ([near], "aM")):
+        if grp is same:
+            done("v", v.memset(T.nxt[:, ZW:ZV], 0.0))
         need("v", [(ar, len(off))])
         for c in grp:
-            x = top(full if c == near[-1] else acc, acc, part(R(c)), x)
+            x = top(full if c == near else acc, acc, part(R(c)), x)
     x = both(lambda c: v.tensor_scalar(T.tgt[:, c], T.acc[:, c], 4095, None, A.bitwise_and), x)
     need("v", x[1] + [s_k])
 
@@ -297,6 +300,15 @@ def rank_program(g, core, T, topo):
 
     def fit(ca, cb):
         return done("v", v.tensor_tensor(T.eq[:, 16 * ca:16 * cb], T.tgt[:].indirect(T.lst[:, ca:cb]), T.kk[:, 16 * ca:16 * cb], A.is_equal))
+
+    need("s", x[1])
+    lent = [done("s", s.activation(T.kk[:, 16 * ca:16 * cb], T.tgt[:].indirect(T.lst[:, ca:cb]), AF.Identity, bias=col(10), scale=1.0))
+            for ca, cb in LENT]
+
+    def match(n):
+        ca, cb = LENT[n]
+        need("v", [lent[n], pk[2 + n]])
+        return done("v", v.tensor_tensor(T.eq[:, 16 * ca:16 * cb], T.kk[:, 16 * ca:16 * cb], T.psB[:, kept(n)], A.is_equal))
 
     def fold(n, e):
         ca, cb = PIECES[n]
@@ -321,32 +333,50 @@ def rank_program(g, core, T, topo):
         scatter("s", n)
 
     fold(0, fit(*PIECES[0]))
-    fit(PIECES[1][0], CUT)
+    fit(va, PIECES[1][1])
+    fold(1, match(0))
     place(0)
-    fold(1, fit(CUT, PIECES[1][1]))
-    fold(2, fit(*PIECES[2]))
+    fit(PIECES[2][0], vb)
+    fold(2, match(1))
     place(1)
     scatter("v", 1)
     place(2)
     scatter("v", 2)
+    for i in range(Q):
+        done("s", s.activation(T.kvw[:, i * W:i * W + Z], T.strip[:, 0:Z], AF.Identity, scale=0.0))
 
     def collect(d, h, dep):
         need("p", [dep])
         for u in range(2):
             b = mdc(d, h) + 16 * u
-            end = d == D - 1 and h == 1 and u == 1
+            end = d == EARLY - 1 and h == 1 and u == 1
             ins = t.matmul(T.psB[:, 16 * h:16 * h + 16], T.fh[:, 15 - d:143 - d], T.md[:, b:b + 16], False, end)
         return done("p", ins) if end else None
 
-    def keys(q, c, sa, sb, dep):
+    def keys(q, c, o, lst, deps):
         i = member(c)
-        need(q, [("ldk%d" % i, 16), dep] + ([("li%d" % i, len(off))] if c is not None else []))
-        src, b = (T.lu, 0) if c is None else (T.lists, S * i)
-        win = T.kvw[:, i * W:(i + 1) * W].indirect(src[:, b + sa:b + sb])
-        o = T.ysb[:, D * (S * i + sa):D * (S * i + sb)]
+        need(q, [("ldk%d" % i, 16)] + deps)
+        win = T.kvw[:, i * W:(i + 1) * W].indirect(lst)
         return done(q, s.activation(o, win, AF.Copy) if q == "s" else v.tensor_copy(o, win))
 
-    need("p", [v_m0[0], v_fh, v_k, s_k])
+    def early(q, c, sa, sb, dep):
+        i = member(c)
+        src, b = (T.lu, 0) if c is None else (T.lists, S * i)
+        return keys(q, c, T.ysb[:, D * (S * i + sa):D * (S * i + sb)], src[:, b + sa:b + sb],
+                    [dep if c is None else ("li%d" % i, len(off))])
+
+    def late(q, c, n, deps):
+        i = member(c)
+        src, b = (T.tail, 64) if c is None else (T.tails, 16 * i)
+        return keys(q, c, T.ysb[:, 512 * i + LATE[n]:512 * (i + 1):D], src[:, b + 2 * n:b + 2 * n + 2],
+                    deps + ([] if c is None else [("lj%d" % i, len(off))]))
+
+    def tell(src, dst, sem):
+        g.remote_dma_fused([RemoteDMATransfer(dst_ids=[dst_id(c) for c in heads], dma_engine_mask=bits(off),
+                                              remote_sem=T.sem[sem % me], srcs=[src], dsts=[dst for c in heads], alu_op=0)],
+                           local_sem=T.sem.lsent)
+
+    need("p", [v_m0[0], v_fh, s_k])
     t.matmul(T.psB[:, 0:32], T.fh[:, 15:143], T.md[:, 0:32], True, False)
     need("v", [scat["s"], scat["v"]])
     for d in range(1, D):
@@ -355,25 +385,41 @@ def rank_program(g, core, T, topo):
             need("v", [last[h]])
             b, m = lcol(d - 1, h), mdc(d, h)
             xs.append(done("v", v.tensor_tensor(T.md[:, m:m + 32], T.nxt[:, 0:TB + W].indirect(T.offw[:, b:b + 2]), T.mask[:], A.mult)))
-            p_l = collect(d, h, xs[h])
-        if d < D - 1:
-            for h in range(2):
-                need("v", [xs[h]])
-                b, m = lcol(d, h), mdc(d, h)
+            if d < EARLY:
+                p_l = collect(d, h, xs[h])
+        if d == EARLY:
+            need("v", [p_l])
+            v_lu = done("v", v.tensor_scalar(T.lu[:], T.psB[:, 0:32], float(Z - 1), None, A.add))
+            need("g", [v_lu])
+            tell(T.lu[:], T.lists[:, me * S:(me + 1) * S], "li%d")
+            need("s", [("ss", count["s"])])
+            s_own = early("s", None, 0, S, v_lu)
+        if d == D - 1:
+            b = lcol(EARLY, 0)
+            done("v", v.tensor_scalar(T.tail[:, 66:64 + NL], T.offw[:, b:lcol(d, 0):OW], float(Z - 1), None, A.add))
+        for h in range(2):
+            need("v", [xs[h]])
+            b, m = lcol(d, h), mdc(d, h)
+            if d < D - 1:
                 last[h] = done("v", v.tensor_tensor_scan(T.offw[:, b - 31:b + 2], T.res[:, 0:33], T.md[:, m:m + 33], 0.0, A.mult, A.add))
-    need("v", [p_l])
-    v_lu = done("v", v.tensor_scalar(T.lu[:], T.psB[:, 0:32], float(Z - 1), None, A.add))
+            else:
+                v_tail = done("v", v.tensor_tensor_scan(T.tail[:, 2 + h:66:2], T.res[:, 0:32], T.md[:, m:m + 32], float(Z - 1), A.mult, A.add))
+    need("g", [v_tail])
+    tell(T.tail[:, 64:64 + NL], T.tails[:, me * 16:me * 16 + NL], "lj%d")
 
-    need("g", [v_lu])
-    mine = T.lists[:, me * S:(me + 1) * S]
-    g.remote_dma_fused([RemoteDMATransfer(dst_ids=[dst_id(c) for c in heads], dma_engine_mask=bits(off), remote_sem=T.sem["li%d" % me],
-                                          srcs=[T.lu[:]], dsts=[mine for c in heads], alu_op=0)], local_sem=T.sem.lsent)
+    stores = []
 
-    for c in order:
-        i = member(c)
-        e1 = keys("v", c, 0, S // 2, v_lu)
-        e2 = keys("s", c, S // 2, S, v_lu)
-        need("y", [e1, e2])
-        g.sync.dma_start(T.y[:, i * 512:(i + 1) * 512], T.ysb[:, i * 512:(i + 1) * 512]).then_inc(T.sem.stored, 16)
-    need("g", [("lsent", len(off)), ("gs", count["g"]), ("ps", count["p"])])
-    need("y", [("stored", 16 * Q)])
+    def store(cs, deps):
+        i, j = min(member(c) for c in cs), max(member(c) for c in cs) + 1
+        assert j - i == len(cs)
+        need("y", deps)
+        g.sync.dma_start(T.y[:, i * 512:j * 512], T.ysb[:, i * 512:j * 512]).then_inc(T.sem.stored, 16)
+        stores.append(cs)
+
+    store([None], [late("vs"[n % 2], None, n, [v_tail, s_own]) for n in range(len(LATE))])
+    base = {c: [early("v", c, 0, S // 2, None), early("s", c, S // 2, S, None)] for c in order[1:]}
+    ends = [[late("vs"[(n + k) % 2], c, n, base[c]) for n in range(len(LATE))] for k, c in enumerate(order[1:])]
+    for c, e in zip(order[1:], ends):
+        store([c], e)
+    need("g", [("lsent", 2 * len(off)), ("gs", count["g"]), ("ps", count["p"])])
+    need("y", [("stored", 16 * len(stores))])

from concourse.bass import DstId, RemoteDMATransfer
from concourse.mybir import AluOpType as A, ActivationFunctionType as AF

M, S, D, Q = 2048, 32, 16, 4
Z = 16
W = M + Z
PIECES = [(58, 72), (2, 58), (72, 128)]
OWN = (34, 96)
LENT = [(2, 34), (96, 128)]
SCAL = [(58, 72), (2, 30), (100, 128)]
VECT = [None, (30, 58), (72, 100)]
DV = 16 * 28
TB = W + DV
EARLY = 13
LATE = [D - 1] + list(range(EARLY, D - 1))
NL = 2 * len(LATE)
MW, OW = 48, 34

SCRATCH = {
    "dsc": ("dram", [8, 128, 128], "int32"),
    "swap": ("dram", [128, 128], "int32"),
    "land": ("sbuf", [128, 1024], "int32"),
    "parw": ("sbuf", [128, 128], "int32"),
    "tokc": ("sbuf", [128, 128], "int32"),
    "it1": ("sbuf", [128, 128], "int32"),
    "it2": ("sbuf", [128, 128], "int32"),
    "acc": ("sbuf", [128, 128], "int32"),
    "tgt": ("sbuf", [128, 128], "int32"),
    "pcol": ("sbuf", [128, 1], "int32"),
    "pi": ("sbuf", [128, 4], "int32"),
    "cst": ("sbuf", [128, 16], "float32"),
    "pair": ("sbuf", [128, 1], "bfloat16"),
    "mg": ("sbuf", [128, 128], "bfloat16"),
    "strip": ("sbuf", [128, 144], "float32"),
    "em": ("sbuf", [128, 1024], "float16"),
    "fm": ("sbuf", [128, 144], "bfloat16"),
    "fh": ("sbuf", [128, 144], "float16"),
    "tok4": ("sbuf", [128, 4, 32], "float16"),
    "tokt": ("sbuf", [128, 128], "float16"),
    "hiw": ("sbuf", [128, 256], "float16"),
    "mix": ("sbuf", [128, 256], "float16"),
    "lst": ("sbuf", [128, 128], "uint16"),
    "pars": ("sbuf", [128, 128], "float32"),
    "kk": ("sbuf", [128, 2048], "float32"),
    "eq": ("sbuf", [128, 2048], "bfloat16"),
    "offu": ("sbuf", [128, 128], "uint16"),
    "vals": ("sbuf", [128, 2048], "float32"),
    "nxt": ("sbuf", [128, TB + W + M], "float32"),
    "c16": ("sbuf", [128, 128], "bfloat16"),
    "arow": ("sbuf", [128, 128], "bfloat16"),
    "ones": ("sbuf", [128, 128], "bfloat16"),
    "mask": ("sbuf", [128, 32], "float32"),
    "res": ("sbuf", [128, 48], "bfloat16"),
    "md": ("sbuf", [128, MW * 2 * D], "float16"),
    "offw": ("sbuf", [128, OW * 2 * D], "uint16"),
    "lu": ("sbuf", [128, 32], "uint16"),
    "lists": ("sbuf", [128, 32 * Q], "uint16"),
    "tail": ("sbuf", [128, 80], "uint16"),
    "tails": ("sbuf", [128, 16 * Q], "uint16"),
    "kvw": ("sbuf", [128, W * Q], "bfloat16"),
    "ysb": ("sbuf", [128, 512 * Q], "bfloat16"),
    "psA": ("psum", [128, 2048], "float32"),
    "psB": ("psum", [128, 2048], "float32"),
}
SEMAPHORES = ["vs", "ss", "ps", "gs", "ldD", "ldX", "ldS", "ldM", "ldP", "ldO", "ldpar", "ldtok", "ldk0", "ldk1", "ldk2", "ldk3",
              "sent", "aD", "aS", "aM", "aP", "aX", "lsent", "stored", "li0", "li1", "li2", "li3", "lj0", "lj1", "lj2", "lj3"]


def rank_program(g, core, T, topo):
    rank = T.rank_of(core)
    if rank is None:
        return
    eng = {"v": g.vector, "s": g.scalar, "p": g.tensor, "g": g, "y": g.sync}
    semof = {"v": "vs", "s": "ss", "p": "ps", "g": "gs"}
    count = {"v": 0, "s": 0, "p": 0, "g": 0}
    seen = {}

    def need(q, deps):
        for name, val in deps:
            if seen.get((q, name), 0) < val:
                eng[q].wait_ge(T.sem[name], int(val))
                seen[(q, name)] = val

    def done(q, ins):
        count[q] += 1
        ins.then_inc(T.sem[semof[q]], 1)
        return (semof[q], count[q])

    chip = topo.chip(core)
    same, mate, plane, diag = [], [], [], []
    for c in T.cores:
        if c == core:
            continue
        oc = topo.chip(c)
        if oc == chip:
            same.append(c)
        elif topo.mates(chip, oc):
            mate.append(c)
        elif topo.same_plane(chip, oc):
            plane.append(c)
        else:
            diag.append(c)
    off = topo.engines(core, diag[0])
    half = len(off) // 2
    bits = lambda es: sum(1 << e for e in es)
    inner = [e for e in topo.engines(core, same[0]) if e not in off]

    def dst_id(c):
        a = topo.addr(c)
        return DstId(rid=a[0], pnc=a[1])

    slot = lambda r: T.land[:, r * 128:(r + 1) * 128]
    piece = lambda r: T.best[:, r * M:(r + 1) * M]
    blk = lambda k: slice(k * 128, (k + 1) * 128)
    R = T.rank_of

    stage = lambda q, c, sem: q.dma_start(T.dsc[R(c)], piece(R(c))).then_inc(T.sem[sem], 16)
    ondie = lambda grp, yes: [c for c in grp if (topo.die(c) == topo.die(core)) == yes][0]
    near, far = ondie(diag, True), ondie(diag, False)
    first, second = ([ondie(plane, yes), ondie(mate, yes)] for yes in (False, True))
    stage(g.sync, first[0], "ldD")
    stage(g.scalar, first[1], "ldD")
    stage(g.sync, far, "ldX")
    for c in second:
        stage(g.sync, c, "ldS")
    stage(g.sync, near, "ldM")
    stage(g.sync, same[0], "ldP")
    g.sync.dma_start(slot(rank), piece(rank)).then_inc(T.sem.ldO, 16)
    for u in range(2):
        g.scalar.dma_start(T.tokc[:, 64 * u:64 * u + 64], T.tok[u::2, :]).then_inc(T.sem.ldtok, 16)
    g.scalar.dma_start(T.parw[:], T.par[:]).then_inc(T.sem.ldpar, 16)

    loose = dict(allow_small_or_imprecise_dtypes=True)
    i_p = done("g", g.iota(T.pcol[:], [[1, 1]], 0, 1))
    i_mg = done("g", g.iota(T.mg[:], [[8, 8], [0, 16]], 0, 0, **loose))
    i_strip = done("g", g.iota(T.strip[:], [[1, 144]], 0, 0, **loose))
    def send(moves):
        g.remote_dma_fused([RemoteDMATransfer(dst_ids=[dst_id(c)], dma_engine_mask=bits(es), remote_sem=T.sem[ar], srcs=srcs,
                                              dsts=[dst], alu_op=2 if len(srcs) > 1 else 0)
                            for c, es, ar, srcs, dst in moves], local_sem=T.sem.sent)

    pair = lambda grp, ar: [(c, off[k * half:(k + 1) * half], ar, [T.dsc[R(c)]], slot(rank)) for k, c in enumerate(grp)]
    need("g", [("ldD", 32)])
    send(pair(first, "aD"))
    need("g", [("ldX", 16)])
    send([(same[0], inner, "aX", [T.dsc[R(far)]], T.swap[:])])
    need("g", [("ldS", 32)])
    send(pair(second, "aS"))
    need("g", [("ldP", 16)])
    send([(same[0], inner, "aP", [T.dsc[R(same[0])]], slot(rank))])
    need("g", [("ldM", 16), ("aX", len(inner))])
    send([(near, off, "aM", [T.dsc[R(near)], T.swap[:]], slot(rank))])
    for ca, cb in SCAL + VECT[1:]:
        done("g", g.iota(T.c16[:, ca:cb], [[16, cb - ca]], W, 0, **loose))
    i_ar = done("g", g.iota(T.arow[:], [[0, 8], [1, 16]], 0, 0, **loose))
    i_val = {}
    for ca, cb in (SCAL[0], SCAL[1], VECT[1], VECT[2], SCAL[2]):
        i_val[ca] = done("g", g.iota(T.vals[:, 16 * ca:16 * cb], [[1, 16 * (cb - ca)]], 1 + 16 * ca, 0, **loose))

    me = rank // 2
    heads = [c for c in diag + mate + plane if R(c) % 2 == rank % 2]
    order = [None] + [c for c in mate + diag + plane if c in heads]
    member = lambda c: me if c is None else R(c) // 2
    need("y", [("sent", 3 * len(off) + 2 * len(inner))])
    for c in order:
        i = member(c)
        g.sync.dma_start(T.kvw[:, i * W + Z:(i + 1) * W], T.kv[:, i * M:(i + 1) * M]).then_inc(T.sem["ldk%d" % i], 16)

    v, t, s = g.vector, g.tensor, g.scalar
    col = lambda k: T.cst[:, k:k + 1]
    icol = lambda k: T.pi[:, k:k + 1]

    ZW, ZV = 256, 896
    v_z = done("v", v.memset(T.nxt[:, TB:TB + ZW], 0.0))
    need("v", [i_p])
    ph = done("v", v.tensor_scalar(icol(0), T.pcol[:], 1, None, A.arith_shift_right))
    po = done("v", v.tensor_scalar(icol(1), T.pcol[:], 1, None, A.bitwise_and))
    pa = done("v", v.tensor_scalar(icol(2), T.pcol[:], 15, None, A.bitwise_and))
    pg = done("v", v.tensor_scalar(icol(3), T.pcol[:], 112, None, A.bitwise_and))
    need("v", [ph])
    c0 = done("v", v.tensor_copy(T.pair[:], icol(0)))
    need("v", [po])
    done("v", v.tensor_scalar(col(1), icol(1), 32.0, -32.0, A.mult, A.add))
    done("v", v.tensor_scalar(col(2), icol(1), 6144.0, -2048.0, A.mult, A.add))
    need("v", [c0, i_mg])
    for q in range(8):
        done("v", v.tensor_scalar(T.em[:, blk(q)], T.mg[:], float(q), T.pair[:], A.add, A.is_equal))
    need("v", [pg])
    done("v", v.tensor_scalar(col(3), icol(1), -32.0, None, A.mult))
    done("v", v.tensor_scalar(col(4), icol(1), -6144.0, 4096.0, A.mult, A.add))
    kb = done("v", v.tensor_scalar(col(5), icol(2), 4096.0, 4096.0, A.mult, A.add))
    done("v", v.tensor_scalar(col(6), icol(3), 15.0, None, A.add))
    done("v", v.tensor_scalar(col(10), icol(2), -4096.0, -4096.0, A.mult, A.add))
    done("v", v.memset(T.nxt[:, 0:ZW], 0.0))

    need("v", [("ldtok", 32)])
    for u in range(2):
        for e in range(2):
            x = done("v", v.tensor_scalar(T.tok4[:, :, 16 * u + 1 - e:16 * u + 16:2], T.tokc[:, 64 * u + e:64 * u + 64:2],
                                          -2048.0, None, A.add))
    need("v", [("ldpar", 16)])
    x1 = done("v", v.tensor_scalar(T.it1[:], T.parw[:], 1920, None, A.bitwise_and))
    need("v", [x])
    for b in range(4):
        done("v", v.transpose(T.tokt[:, 32 * b:32 * b + 32], T.tok4[:, b, :]))
    v_mix = []
    need("v", [x1])
    hs = [done("v", v.tensor_scalar(T.hiw[:, blk(e)], T.it1[:], col(1 + 2 * e), col(2 + 2 * e), A.mult, A.add)) for e in range(2)]
    for e in range(2):
        need("v", [hs[e]])
        for b in range(4):
            cs = slice(128 * e + b, 128 * e + 128, 4)
            x = done("v", v.tensor_tensor(T.mix[:, cs], T.tokt[:, 32 * b:32 * b + 32], T.hiw[:, cs], A.min))
        v_mix.append(x)
    x2 = done("v", v.tensor_scalar(T.it2[:], T.parw[:], 127, None, A.bitwise_and))
    done("v", v.tensor_scalar(T.pars[:], T.parw[:], 1.0, None, A.add))
    need("v", [x2, i_strip])
    done("v", v.tensor_copy(T.lst[:], T.it2[:]))
    v_ones = done("v", v.memset(T.ones[:], 1.0 / 128))
    v_f = done("v", v.tensor_scalar(T.fm[:], T.strip[:], col(6), -8192.0, A.is_equal, A.mult))
    v_fh = done("v", v.tensor_scalar(T.fh[:], T.strip[:], col(6), None, A.is_equal))

    ks = [2 * q + e for e in range(2) for q in range(8)]
    va, vb = OWN
    kps = lambda n: T.psB[:, 64 * n:64 * n + vb - va]
    kept = lambda n: slice(512 * (2 + n), 512 * (3 + n))
    mix = lambda k, ca, cb: T.mix[:, 128 * (k % 2) + ca:128 * (k % 2) + cb]
    pk = []
    for n, k in enumerate(ks):
        need("p", [v_mix[k % 2]])
        ins = t.matmul(kps(n), T.em[:, blk(k // 2)], mix(k, va, vb), True, True)
        if n % 8 == 7:
            pk.append(done("p", ins))
    for n, (ca, cb) in enumerate(LENT):
        for k in ks:
            ins = t.matmul(T.psB[:, kept(n).start + k:kept(n).stop:16], T.em[:, blk(k // 2)], mix(k, ca, cb), True, True)
        pk.append(done("p", ins))
    need("p", [v_f, i_ar])
    for n, (ca, cb) in enumerate(PIECES):
        ps = T.psA[:, n * 512:n * 512 + cb - ca]
        t.matmul(ps, T.ones[:], T.c16[:, ca:cb], True, False)
        t.matmul(ps, T.arow[:], T.ones[:, 0:cb - ca], False, False)

    zeros = lambda n: T.nxt[:, TB:TB + n]
    need("s", [v_z])
    done("s", s.activation(T.nxt[:, TB + M:TB + W], zeros(Z), AF.Silu, scale=0.0))
    for j in range(TB + ZW, TB + M, ZW):
        x = done("s", s.activation(T.nxt[:, j:j + ZW], zeros(ZW), AF.Identity))
    done("s", s.activation(T.nxt[:, ZV:ZV + ZW], zeros(ZW), AF.Identity))
    for n, k in enumerate(ks):
        need("s", [pk[n // 8], kb])
        s_k = done("s", s.activation(T.kk[:, 16 * va + k:16 * vb:16], kps(n), AF.Identity, bias=col(5), scale=1.0))
    need("s", [x])
    s_zero = done("s", s.activation(T.nxt[:, ZV + ZW:TB], zeros(TB - ZV - ZW), AF.Identity))

    def both(op, deps=((), ())):
        out = []
        for h in range(2):
            need("v", deps[h])
            out.append([done("v", op(slice(64 * h, 64 * h + 64)))])
        return out

    def top(o, p, q, deps=((), ())):
        return both(lambda c: v.tensor_tensor(o(c), p(c), q(c), A.max), deps)

    mdc = lambda d, h: MW * (2 * d + h)
    lcol = lambda d, h: OW * (2 * d + h) + 32
    last, v_m0 = [], []

    def walk_tiles():
        x = done("v", v.tensor_copy(col(7), icol(2)))
        ys = [done("v", v.tensor_scalar(col(8 + h), icol(2), float(1 + 16 * h), None, A.add)) for h in range(2)]
        done("v", v.memset(T.res[:], 1.0))
        done("v", v.tensor_scalar(T.md[:, 32::MW], T.strip[:, 0:2 * D], 0.0, float(TB), A.mult, A.add))
        need("v", [x])
        for h in range(2):
            x = done("v", v.tensor_scalar(T.mask[:, 16 * h:16 * h + 16], T.strip[:, 0:16], col(7), None, A.is_equal))
        need("v", ys)
        for h in range(2):
            b = lcol(0, h)
            last.append(done("v", v.tensor_scalar(T.offw[:, b:b + 2], T.strip[:, 0:2], float(TB), col(8 + h), A.mult, A.add)))
        need("v", [x])
        v_m0.append(done("v", v.tensor_tensor(T.md[:, 0:32], T.mask[:], T.strip[:, 1:33], A.mult)))

    part = lambda r: (lambda c: T.land[:, r * 128 + c.start:r * 128 + c.stop])
    acc, full = (lambda c: T.psA[:, 1536 + c.start:1536 + c.stop]), (lambda c: T.acc[:, c])
    walk_tiles()
    need("v", [("ldO", 16), ("aD", len(off))])
    x = top(acc, part(rank), part(R(first[0])))
    for grp, ar in ((first[1:], "aD"), (same, "aP"), (second, "aS"), ([near], "aM")):
        if grp is same:
            done("v", v.memset(T.nxt[:, ZW:ZV], 0.0))
        need("v", [(ar, len(off))])
        for c in grp:
            x = top(full if c == near else acc, acc, part(R(c)), x)
    x = both(lambda c: v.tensor_scalar(T.tgt[:, c], T.acc[:, c], 4095, None, A.bitwise_and), x)
    need("v", x[1] + [s_k])

    p_ok, placed = [], []

    def fit(ca, cb):
        return done("v", v.tensor_tensor(T.eq[:, 16 * ca:16 * cb], T.tgt[:].indirect(T.lst[:, ca:cb]), T.kk[:, 16 * ca:16 * cb], A.is_equal))

    need("s", x[1])
    lent = [done("s", s.activation(T.kk[:, 16 * ca:16 * cb], T.tgt[:].indirect(T.lst[:, ca:cb]), AF.Identity, bias=col(10), scale=1.0))
            for ca, cb in LENT]

    def match(n):
        ca, cb = LENT[n]
        need("v", [lent[n], pk[2 + n]])
        return done("v", v.tensor_tensor(T.eq[:, 16 * ca:16 * cb], T.kk[:, 16 * ca:16 * cb], T.psB[:, kept(n)], A.is_equal))

    def fold(n, e):
        ca, cb = PIECES[n]
        need("p", [e])
        for k in range(16):
            ins = t.matmul(T.psA[:, n * 512:n * 512 + cb - ca], T.fm[:, 15 - k:143 - k], T.eq[:, 16 * ca + k:16 * cb:16], False, k == 15)
        p_ok.append(done("p", ins))

    scat = {"s": s_zero, "v": s_zero}

    def scatter(q, n):
        ca, cb = (SCAL if q == "s" else VECT)[n]
        need(q, [placed[n], i_val[ca], scat[q]])
        src, o = T.vals[:, 16 * ca:16 * cb], T.offu[:, ca:cb]
        scat[q] = done(q, s.activation(T.nxt[:, TB:TB + W + M].indirect(o), src, AF.Silu) if q == "s"
                       else v.tensor_copy(T.nxt[:, 0:TB].indirect(o), src))

    def place(n):
        ca, cb = PIECES[n]
        need("v", [p_ok[n]])
        placed.append(done("v", v.tensor_tensor(T.offu[:, ca:cb], T.psA[:, n * 512:n * 512 + cb - ca], T.pars[:, ca:cb], A.max)))
        scatter("s", n)

    fold(0, fit(*PIECES[0]))
    fit(va, PIECES[1][1])
    fold(1, match(0))
    place(0)
    fit(PIECES[2][0], vb)
    fold(2, match(1))
    place(1)
    scatter("v", 1)
    place(2)
    scatter("v", 2)
    for i in range(Q):
        done("s", s.activation(T.kvw[:, i * W:i * W + Z], T.strip[:, 0:Z], AF.Identity, scale=0.0))

    def collect(d, h, dep):
        need("p", [dep])
        for u in range(2):
            b = mdc(d, h) + 16 * u
            end = d == EARLY - 1 and h == 1 and u == 1
            ins = t.matmul(T.psB[:, 16 * h:16 * h + 16], T.fh[:, 15 - d:143 - d], T.md[:, b:b + 16], False, end)
        return done("p", ins) if end else None

    def keys(q, c, o, lst, deps):
        i = member(c)
        need(q, [("ldk%d" % i, 16)] + deps)
        win = T.kvw[:, i * W:(i + 1) * W].indirect(lst)
        return done(q, s.activation(o, win, AF.Copy) if q == "s" else v.tensor_copy(o, win))

    def early(q, c, sa, sb, dep):
        i = member(c)
        src, b = (T.lu, 0) if c is None else (T.lists, S * i)
        return keys(q, c, T.ysb[:, D * (S * i + sa):D * (S * i + sb)], src[:, b + sa:b + sb],
                    [dep if c is None else ("li%d" % i, len(off))])

    def late(q, c, n, deps):
        i = member(c)
        src, b = (T.tail, 64) if c is None else (T.tails, 16 * i)
        return keys(q, c, T.ysb[:, 512 * i + LATE[n]:512 * (i + 1):D], src[:, b + 2 * n:b + 2 * n + 2],
                    deps + ([] if c is None else [("lj%d" % i, len(off))]))

    def tell(src, dst, sem):
        g.remote_dma_fused([RemoteDMATransfer(dst_ids=[dst_id(c) for c in heads], dma_engine_mask=bits(off),
                                              remote_sem=T.sem[sem % me], srcs=[src], dsts=[dst for c in heads], alu_op=0)],
                           local_sem=T.sem.lsent)

    need("p", [v_m0[0], v_fh, s_k])
    t.matmul(T.psB[:, 0:32], T.fh[:, 15:143], T.md[:, 0:32], True, False)
    need("v", [scat["s"], scat["v"]])
    for d in range(1, D):
        xs = []
        for h in range(2):
            need("v", [last[h]])
            b, m = lcol(d - 1, h), mdc(d, h)
            xs.append(done("v", v.tensor_tensor(T.md[:, m:m + 32], T.nxt[:, 0:TB + W].indirect(T.offw[:, b:b + 2]), T.mask[:], A.mult)))
            if d < EARLY:
                p_l = collect(d, h, xs[h])
        if d == EARLY:
            need("v", [p_l])
            v_lu = done("v", v.tensor_scalar(T.lu[:], T.psB[:, 0:32], float(Z - 1), None, A.add))
            need("g", [v_lu])
            tell(T.lu[:], T.lists[:, me * S:(me + 1) * S], "li%d")
            need("s", [("ss", count["s"])])
            s_own = early("s", None, 0, S, v_lu)
        if d == D - 1:
            b = lcol(EARLY, 0)
            done("v", v.tensor_scalar(T.tail[:, 66:64 + NL], T.offw[:, b:lcol(d, 0):OW], float(Z - 1), None, A.add))
        for h in range(2):
            need("v", [xs[h]])
            b, m = lcol(d, h), mdc(d, h)
            if d < D - 1:
                last[h] = done("v", v.tensor_tensor_scan(T.offw[:, b - 31:b + 2], T.res[:, 0:33], T.md[:, m:m + 33], 0.0, A.mult, A.add))
            else:
                v_tail = done("v", v.tensor_tensor_scan(T.tail[:, 2 + h:66:2], T.res[:, 0:32], T.md[:, m:m + 32], float(Z - 1), A.mult, A.add))
    need("g", [v_tail])
    tell(T.tail[:, 64:64 + NL], T.tails[:, me * 16:me * 16 + NL], "lj%d")

    stores = []

    def store(cs, deps):
        i, j = min(member(c) for c in cs), max(member(c) for c in cs) + 1
        assert j - i == len(cs)
        need("y", deps)
        g.sync.dma_start(T.y[:, i * 512:j * 512], T.ysb[:, i * 512:j * 512]).then_inc(T.sem.stored, 16)
        stores.append(cs)

    store([None], [late("vs"[n % 2], None, n, [v_tail, s_own]) for n in range(len(LATE))])
    base = {c: [early("v", c, 0, S // 2, None), early("s", c, S // 2, S, None)] for c in order[1:]}
    ends = [[late("vs"[(n + k) % 2], c, n, base[c]) for n in range(len(LATE))] for k, c in enumerate(order[1:])]
    for c, e in zip(order[1:], ends):
        store([c], e)
    need("g", [("lsent", 2 * len(off)), ("gs", count["g"]), ("ps", count["p"])])
    need("y", [("stored", 16 * len(stores))])
